import numpy as np
import ml_dtypes


def mxq(x, axis, fmt="e4m3"):
    dtype, down = {"e4m3": (ml_dtypes.float8_e4m3fn, 7), "e5m2": (ml_dtypes.float8_e5m2, 14)}[fmt]
    v = np.moveaxis(np.asarray(x, np.float32).astype(ml_dtypes.bfloat16).astype(np.float64), axis, -1)
    blocks = v.reshape(v.shape[:-1] + (-1, 32))
    amax = np.abs(blocks).max(-1, keepdims=True)
    byte = np.maximum(np.where(amax > 0, np.frexp(amax)[1] - 1 + 127, 0) - down, 1)
    scale = np.exp2(byte - 127.0)
    codes = (blocks / scale).astype(np.float32).astype(dtype).astype(np.float64)
    return np.moveaxis((codes * scale).reshape(v.shape), -1, axis)


WIDE = False


def mx_kscale(k):
    if not WIDE:
        return np.ones(k)
    levels = np.array([10, -10, 5, -5, 0])
    if k % 512:
        return np.exp2(np.random.permutation(np.resize(levels, k // 32))).repeat(32)
    a = np.empty((k // 512, 16))
    for p in range(k // 512):
        a[p, :8] = np.random.permutation(np.resize(levels, 8))
        for g in range(8):
            far = levels[np.abs(levels - a[p, g]) >= 10]
            a[p, g + 8] = far[np.random.randint(len(far))]
    return np.exp2(a.ravel()).repeat(32)


def f64(x):
    return np.asarray(x).astype(np.float64)


E2M1 = np.array([0.0, 0.5, 1.0, 1.5, 2.0, 3.0, 4.0, 6.0, -0.0, -0.5, -1.0, -1.5, -2.0, -3.0, -4.0, -6.0])


def pack_weight(w, fmt):
    k, n = w.shape
    w = f64(np.asarray(w, np.float32).astype(ml_dtypes.bfloat16)).reshape(k // 32, 32, n)
    amax = np.abs(w).max(1)
    if fmt == "e4m3":
        byte = np.frexp(amax)[1] - 1 + 127 - 7
    else:
        mant, ex = np.frexp(amax / 6.0)
        byte = np.where(mant > 0.5, ex, ex - 1) + 127
    byte = np.clip(np.where(amax > 0, byte, 1), 1, 254)
    scaled = (w * np.exp2(127.0 - byte)[:, None, :]).reshape(k, n).astype(np.float32)
    by_word = np.ascontiguousarray(scaled.reshape(k // 512, 128, 4, n).transpose(0, 1, 3, 2))
    if fmt == "e4m3":
        words = by_word.astype(ml_dtypes.float8_e4m3fn).view(np.uint8)
    else:
        c = by_word.astype(ml_dtypes.float4_e2m1fn).view(np.uint8) & 0xF
        words = (c[..., 0::2] | (c[..., 1::2] << 4)).reshape(k // 512, 128, 2 * n)
    return np.ascontiguousarray(words), np.ascontiguousarray(byte.astype(np.uint8).reshape(k // 512, 16, n))


def unpack_weight(words, scales, fmt):
    g, _, n = scales.shape
    words = np.ascontiguousarray(words).reshape(g, 128, n, -1)
    if fmt == "e4m3":
        vals = words.view(ml_dtypes.float8_e4m3fn).astype(np.float64)
    else:
        nib = np.empty((g, 128, n, 4), np.uint8)
        nib[..., 0::2] = words & 0xF
        nib[..., 1::2] = words >> 4
        vals = E2M1[nib]
    vals = vals * np.repeat(np.exp2(scales.astype(np.float64) - 127.0), 8, axis=1)[..., None]
    return vals.transpose(0, 1, 3, 2).reshape(g * 512, n)


K, R, M, T = 2048, 512, 1536, 512


def setup_inputs():
    n = np.random.standard_normal
    s = mx_kscale(K)[:, None]
    u = mx_kscale(R)[:, None]
    p_w4 = pack_weight(n((K, M)) / np.sqrt(K) / s, "e2m1")
    return {
        "x": (n((K, T)) * s).astype(np.float32),
        "w4_words": p_w4[0],
        "w4_scales": p_w4[1],
        "down": (n((K, R)) / np.sqrt(K) / s * u.T).astype(np.float32),
        "up": (0.5 * n((R, M)) / np.sqrt(R) / u).astype(np.float32),
        "b": (0.3 * n(1536)).astype(np.float32),
    }


def reference(x, w4_words, w4_scales, down, up, b):
    x_ = mxq(f64(x), 0, "e4m3")
    w4_ = unpack_weight(w4_words, w4_scales, "e2m1")
    down_ = mxq(f64(down), 0, "e4m3")
    up_ = mxq(f64(up), 0, "e4m3")
    h_ = mxq(down_.T @ x_, 0, "e4m3")
    y = w4_.T @ x_ + up_.T @ h_
    return y + f64(b)[:, None]

@@ -1,0 +1,262 @@
+from contextlib import ExitStack
+
+import concourse.mybir as mybir
+from concourse.masks import make_identity
+
+K, R, N, T = 2048, 512, 1536, 512
+FLOPS = 2 * T * (K * R + K * N + R * N)
+
+F32 = mybir.dt.float32
+BF16 = mybir.dt.bfloat16
+I32 = mybir.dt.int32
+U32 = mybir.dt.uint32
+U8 = mybir.dt.uint8
+E4M3X4 = mybir.dt.float8_e4m3fn_x4
+E2M1X4 = mybir.dt.float4_e2m1fn_x4
+IDENTITY = mybir.ActivationFunctionType.Identity
+ADD = mybir.AluOpType.add
+
+P = 128
+PACK = 4
+K_PASS = P * PACK
+PASSES = K // K_PASS
+N_TILES = N // P
+W_COLS = (512, 1024)
+W_LOADS = 3
+U_LOADS = 2
+WL = N // W_LOADS
+UL = N // U_LOADS
+
+X_SPLIT = 352
+DOWN_SPLIT = 88
+UP_SPLIT = 384
+H_SPLIT = 352
+
+
+def tile_mix_lowrank_fm_bias_kernel(tc, x, w4_words, w4_scales, down, up, b, out):
+    nc = tc.nc
+    with ExitStack() as ctx:
+        keep = ctx.enter_context(tc.tile_pool(name="keep", bufs=1))
+        psum = ctx.enter_context(tc.psum_pool(name="psum", bufs=1))
+        ctx.enter_context(tc.manual_schedule())
+
+        def sbuf(name, shape, dtype):
+            return keep.tile(shape, dtype, name=name, align_bytes=64)
+
+        def bank(i, name):
+            return psum.tile([P, T], F32, name=name, tag=f"bank{i}")
+
+        x_raw = [sbuf(f"x_raw{g}", [P, PACK, T], F32) for g in range(PASSES)]
+        x_bf = [sbuf(f"x_bf{g}", [P, T, PACK], BF16) for g in range(PASSES)]
+        x_codes = [sbuf(f"x_codes{g}", [P, T], U32) for g in range(PASSES)]
+        x_scales = [sbuf(f"x_scales{g}", [P, T], U8) for g in range(PASSES)]
+        d_raw = [sbuf(f"d_raw{g}", [P, PACK, R], F32) for g in range(PASSES)]
+        d_bf = [sbuf(f"d_bf{g}", [P, PACK, P, PACK], BF16) for g in range(PASSES)]
+        d_codes = [sbuf(f"d_codes{g}", [P, R], U32) for g in range(PASSES)]
+        d_scales = [sbuf(f"d_scales{g}", [P, R], U8) for g in range(PASSES)]
+        u_raw = [sbuf(f"u_raw{c}", [P, PACK, UL], F32) for c in range(U_LOADS)]
+        u_bf = [sbuf(f"u_bf{c}", [P, UL, PACK], BF16) for c in range(U_LOADS)]
+        u_codes = [sbuf(f"u_codes{c}", [P, UL], U32) for c in range(U_LOADS)]
+        u_scales = [sbuf(f"u_scales{c}", [P, UL], U8) for c in range(U_LOADS)]
+        w_words = [sbuf(f"w_words{c}", [P, PASSES, 2 * WL], U8) for c in range(W_LOADS)]
+        w_scales = [sbuf(f"w_scales{c}", [P, PASSES, n], U8) for c, n in enumerate(W_COLS)]
+        h_sb = sbuf("h_sb", [P, PACK, T], BF16)
+        h_bf = sbuf("h_bf", [P, T, PACK], BF16)
+        h_codes = sbuf("h_codes", [P, T], U32)
+        h_scales = sbuf("h_scales", [P, T], U8)
+        ident = sbuf("ident", [P, P], F32)
+        b_rows = sbuf("b_rows", [P, P], F32)
+        b_cols = sbuf("b_cols", [P, N_TILES], F32)
+        warm = sbuf("warm", [P, 1], F32)
+        y_sb = [sbuf(f"y_sb{i}", [P, T], F32) for i in range(N_TILES)]
+
+        nc.vector.memset(warm[:], 0.0)
+        nc.vector.memset(b_rows[:], 0.0)
+        for c in range(2):
+            nc.vector.memset(w_scales[c][:].rearrange("p g n -> p (g n)").bitcast(I32), 0)
+        make_identity(nc, ident[:])
+
+        def load_rows(tile, rows):
+            nc.sync.dma_start(out=tile[:], in_=rows.rearrange("(p j) w -> p j w", j=PACK))
+
+        def load_w_words(c):
+            nc.sync.dma_start(
+                out=w_words[c][:],
+                in_=w4_words[:, :, 2 * c * WL : 2 * (c + 1) * WL].rearrange("g p n -> p g n"),
+            )
+
+        def load_w_scales(c):
+            cols = slice(sum(W_COLS[:c]), sum(W_COLS[: c + 1]))
+            for r in range(4):
+                nc.sync.dma_start(
+                    out=w_scales[c][r:P:32, :, :].bitcast(I32),
+                    in_=w4_scales[:, r:16:4, cols].rearrange("g q n -> q g n").bitcast(I32),
+                )
+
+        nc.scalar.dma_start(out=b_rows[0:N_TILES, :], in_=b.rearrange("(c p) -> c p", p=P))
+        k_rows = [slice(g * K_PASS, (g + 1) * K_PASS) for g in range(PASSES)]
+        u_cols = [slice(c * UL, (c + 1) * UL) for c in range(U_LOADS)]
+        load_rows(x_raw[0], x[k_rows[0], :])
+        load_rows(d_raw[0], down[k_rows[0], :])
+        load_w_words(0)
+        load_w_scales(0)
+        for g in range(1, PASSES):
+            load_rows(x_raw[g], x[k_rows[g], :])
+            load_rows(d_raw[g], down[k_rows[g], :])
+        load_w_words(1)
+        load_w_scales(1)
+        load_rows(u_raw[0], up[:, u_cols[0]])
+        load_w_words(2)
+        load_rows(u_raw[1], up[:, u_cols[1]])
+
+        def interleave(copy, dst, src, lo, hi):
+            copy(
+                out=dst[:, lo:hi, :].rearrange("p (c i) t -> p c t i", i=4),
+                in_=src[:, :, lo:hi].rearrange("p t (c i) -> p c t i", i=4),
+            )
+
+        def interleave_both(dst, src, split, width):
+            interleave(nc.vector.tensor_copy, dst, src, 0, split)
+            interleave(nc.scalar.copy, dst, src, split, width)
+
+        def permute(copy, g, lo, hi):
+            for t in (0, 2):
+                copy(
+                    out=d_bf[g][:, t : t + 2, lo:hi, :].rearrange("p t m j -> p m j t"),
+                    in_=d_raw[g][:, :, 4 * lo : 4 * hi].rearrange("p j (m t) -> p m j t", t=4)[:, :, :, t : t + 2],
+                )
+
+        def permute_both(g):
+            permute(nc.vector.tensor_copy, g, 0, DOWN_SPLIT)
+            permute(nc.scalar.copy, g, DOWN_SPLIT, P)
+
+        def quantize(codes, scales, grouped):
+            nc.vector.quantize_mx(out=codes.bitcast(E4M3X4), scales=scales, in_=grouped)
+
+        def quantize_rows(codes, scales, grouped):
+            quantize(codes[:], scales[:], grouped[:].rearrange("p w j -> p (w j)"))
+
+        def w4_pass(i, acc, g):
+            c, m = i * P // WL, i * P % WL
+            d, n = (0, i * P) if i * P < W_COLS[0] else (1, i * P - W_COLS[0])
+            nc.tensor.matmul_mx(
+                out=acc,
+                lhsT=w_words[c][:, g, 2 * m : 2 * (m + P)].bitcast(E2M1X4),
+                lhsT_scale=w_scales[d][:, g, n : n + P],
+                rhs=x_codes[g][:].bitcast(E4M3X4),
+                rhs_scale=x_scales[g][:],
+                start=(g == 0),
+                stop=False,
+            )
+
+        def up_pass(i, acc):
+            c, m = i * P // UL, i * P % UL
+            nc.tensor.matmul_mx(
+                out=acc,
+                lhsT=u_codes[c][:, m : m + P].bitcast(E4M3X4),
+                lhsT_scale=u_scales[c][:, m : m + P],
+                rhs=h_codes[:].bitcast(E4M3X4),
+                rhs_scale=h_scales[:],
+                start=False,
+                stop=True,
+            )
+
+        def h_pass(j, acc, g):
+            cols = slice(j * P, (j + 1) * P)
+            nc.tensor.matmul_mx(
+                out=acc[:],
+                lhsT=d_codes[g][:, cols].bitcast(E4M3X4),
+                lhsT_scale=d_scales[g][:, cols],
+                rhs=x_codes[g][:].bitcast(E4M3X4),
+                rhs_scale=x_scales[g][:],
+                start=(g == 0),
+                stop=(g == PASSES - 1),
+            )
+
+        def finish(i, acc, on_vector, ts=slice(0, T)):
+            bias = b_cols[:, i : i + 1]
+            if on_vector:
+                nc.vector.tensor_scalar(out=y_sb[i][:, ts], in0=acc, scalar1=bias, scalar2=None, op0=ADD)
+            else:
+                nc.scalar.activation(out=y_sb[i][:, ts], in_=acc, func=IDENTITY, bias=bias)
+            nc.sync.dma_start(out=out[i * P : (i + 1) * P, ts], in_=y_sb[i][:, ts])
+
+        nc.scalar.activation(out=warm[:], in_=warm[:], func=IDENTITY)
+        b_psum = bank(7, "b_psum")
+        nc.tensor.transpose(b_psum[:, 0:P], b_rows[:], ident[:])
+
+        acc = {}
+        h_acc = [bank(j, f"h{j}") for j in range(PACK)]
+
+        for g in range(PASSES):
+            interleave_both(x_bf[g], x_raw[g], X_SPLIT, T)
+            if g == 0:
+                nc.scalar.copy(out=b_cols[:], in_=b_psum[:, 0:N_TILES])
+                for i in range(4):
+                    acc[i] = bank(4 + i, f"y{i}")
+            quantize_rows(x_codes[g], x_scales[g], x_bf[g])
+            for i in range(4):
+                w4_pass(i, acc[i][:], g)
+            permute_both(g)
+            if g < PASSES - 1:
+                quantize(d_codes[g][:], d_scales[g][:], d_bf[g][:].rearrange("p t m j -> p (t m j)"))
+            else:
+                for j in range(PACK):
+                    cols = slice(j * P, (j + 1) * P)
+                    quantize(d_codes[g][:, cols], d_scales[g][:, cols], d_bf[g][:, j, :, :].rearrange("p m j -> p (m j)"))
+            for j in range(PACK):
+                h_pass(j, h_acc[j], g)
+
+        for j in range(PACK):
+            copy = nc.vector.tensor_copy if j % 2 else nc.scalar.copy
+            copy(out=h_sb[:, j, :], in_=h_acc[j][:])
+        interleave_both(h_bf, h_sb, H_SPLIT, T)
+        quantize_rows(h_codes, h_scales, h_bf)
+
+        def quantize_up(c, lo, hi):
+            quantize(u_codes[c][:, lo:hi], u_scales[c][:, lo:hi], u_bf[c][:, lo:hi, :].rearrange("p w j -> p (w j)"))
+
+        def make_up(c):
+            interleave(nc.scalar.copy, u_bf[c], u_raw[c], UP_SPLIT, 512)
+            interleave(nc.vector.tensor_copy, u_bf[c], u_raw[c], 0, UP_SPLIT)
+            interleave(nc.scalar.copy, u_bf[c], u_raw[c], 640, UL)
+            interleave(nc.vector.tensor_copy, u_bf[c], u_raw[c], 512, 640)
+            quantize_up(c, 0, 512)
+            quantize_up(c, 512, UL)
+
+        def w4_tile(i):
+            acc[i] = bank(i - 4, f"y{i}")
+            for g in range(PASSES):
+                w4_pass(i, acc[i][:], g)
+
+        def up_tile(i):
+            up_pass(i, acc[i][:])
+
+        def out_tile(i, on_vector):
+            finish(i, acc[i][:], on_vector)
+
+        make_up(0)
+        for i in (4, 5, 6, 7):
+            w4_tile(i)
+        for i in range(6):
+            up_tile(i)
+        out_tile(0, False)
+        out_tile(1, True)
+        out_tile(2, False)
+        out_tile(3, True)
+        out_tile(4, False)
+        out_tile(5, True)
+        for i in (8, 9, 10):
+            w4_tile(i)
+        make_up(1)
+        for i in (6, 7, 8, 9, 10):
+            up_tile(i)
+        out_tile(6, False)
+        out_tile(7, True)
+        out_tile(8, False)
+        out_tile(9, True)
+        out_tile(10, False)
+        w4_tile(11)
+        up_tile(11)
+        finish(11, acc[11][:, 0 : T // 2], True, slice(0, T // 2))
+        finish(11, acc[11][:, T // 2 : T], True, slice(T // 2, T))

@@ -21,16 +21,14 @@ PACK = 4
 K_PASS = P * PACK
 PASSES = K // K_PASS
 N_TILES = N // P
-W_COLS = (512, 1024)
-W_LOADS = 3
-U_LOADS = 2
-WL = N // W_LOADS
-UL = N // U_LOADS
+GROUP = 4
+GW = GROUP * P
+PARKED, OPEN, LATE = 0, 1, 2
+TQ = T // PACK
 
 X_SPLIT = 352
 DOWN_SPLIT = 88
 UP_SPLIT = 384
-H_SPLIT = 352
 
 
 def tile_mix_lowrank_fm_bias_kernel(tc, x, w4_words, w4_scales, down, up, b, out):
@@ -54,13 +52,13 @@ def tile_mix_lowrank_fm_bias_kernel(tc, x, w4_words, w4_scales, down, up, b, out
         d_bf = [sbuf(f"d_bf{g}", [P, PACK, P, PACK], BF16) for g in range(PASSES)]
         d_codes = [sbuf(f"d_codes{g}", [P, R], U32) for g in range(PASSES)]
         d_scales = [sbuf(f"d_scales{g}", [P, R], U8) for g in range(PASSES)]
-        u_raw = [sbuf(f"u_raw{c}", [P, PACK, UL], F32) for c in range(U_LOADS)]
-        u_bf = [sbuf(f"u_bf{c}", [P, UL, PACK], BF16) for c in range(U_LOADS)]
-        u_codes = [sbuf(f"u_codes{c}", [P, UL], U32) for c in range(U_LOADS)]
-        u_scales = [sbuf(f"u_scales{c}", [P, UL], U8) for c in range(U_LOADS)]
-        w_words = [sbuf(f"w_words{c}", [P, PASSES, 2 * WL], U8) for c in range(W_LOADS)]
-        w_scales = [sbuf(f"w_scales{c}", [P, PASSES, n], U8) for c, n in enumerate(W_COLS)]
-        h_sb = sbuf("h_sb", [P, PACK, T], BF16)
+        u_raw = [sbuf(f"u_raw{c}", [P, PACK, GW], F32) for c in range(3)]
+        u_bf = [sbuf(f"u_bf{c}", [P, GW, PACK], BF16) for c in range(3)]
+        u_codes = [sbuf(f"u_codes{c}", [P, GW], U32) for c in range(3)]
+        u_scales = [sbuf(f"u_scales{c}", [P, GW], U8) for c in range(3)]
+        w_early = sbuf("w_early", [P, PASSES, 2 * 2 * GW], U8)
+        w_late = sbuf("w_late", [P, PASSES, 2 * GW], U8)
+        w_scales = sbuf("w_scales", [P, PASSES, N], U8)
         h_bf = sbuf("h_bf", [P, T, PACK], BF16)
         h_codes = sbuf("h_codes", [P, T], U32)
         h_scales = sbuf("h_scales", [P, T], U8)
@@ -70,54 +68,43 @@ def tile_mix_lowrank_fm_bias_kernel(tc, x, w4_words, w4_scales, down, up, b, out
         warm = sbuf("warm", [P, 1], F32)
         y_sb = [sbuf(f"y_sb{i}", [P, T], F32) for i in range(N_TILES)]
 
-        nc.vector.memset(warm[:], 0.0)
         nc.vector.memset(b_rows[:], 0.0)
-        for c in range(2):
-            nc.vector.memset(w_scales[c][:].rearrange("p g n -> p (g n)").bitcast(I32), 0)
+        nc.vector.memset(w_scales[:].rearrange("p g n -> p (g n)").bitcast(I32), 0)
+        nc.vector.memset(warm[:], 0.0)
         make_identity(nc, ident[:])
 
         def load_rows(tile, rows):
             nc.sync.dma_start(out=tile[:], in_=rows.rearrange("(p j) w -> p j w", j=PACK))
 
-        def load_w_words(c):
-            nc.sync.dma_start(
-                out=w_words[c][:],
-                in_=w4_words[:, :, 2 * c * WL : 2 * (c + 1) * WL].rearrange("g p n -> p g n"),
-            )
+        def load_w_words(tile, lo, hi):
+            nc.sync.dma_start(out=tile[:], in_=w4_words[:, :, 2 * lo : 2 * hi].rearrange("g p n -> p g n"))
 
-        def load_w_scales(c):
-            cols = slice(sum(W_COLS[:c]), sum(W_COLS[: c + 1]))
+        def load_w_scales():
             for r in range(4):
                 nc.sync.dma_start(
-                    out=w_scales[c][r:P:32, :, :].bitcast(I32),
-                    in_=w4_scales[:, r:16:4, cols].rearrange("g q n -> q g n").bitcast(I32),
+                    out=w_scales[r:P:32, :, :].bitcast(I32),
+                    in_=w4_scales[:, r:16:4, :].rearrange("g q n -> q g n").bitcast(I32),
                 )
 
-        nc.scalar.dma_start(out=b_rows[0:N_TILES, :], in_=b.rearrange("(c p) -> c p", p=P))
         k_rows = [slice(g * K_PASS, (g + 1) * K_PASS) for g in range(PASSES)]
-        u_cols = [slice(c * UL, (c + 1) * UL) for c in range(U_LOADS)]
         load_rows(x_raw[0], x[k_rows[0], :])
-        load_rows(d_raw[0], down[k_rows[0], :])
-        load_w_words(0)
-        load_w_scales(0)
+        nc.scalar.dma_start(out=b_rows[0:N_TILES, :], in_=b.rearrange("(c p) -> c p", p=P))
+        load_w_scales()
+        load_w_words(w_early, 0, 2 * GW)
         for g in range(1, PASSES):
             load_rows(x_raw[g], x[k_rows[g], :])
+        for g in range(PASSES):
             load_rows(d_raw[g], down[k_rows[g], :])
-        load_w_words(1)
-        load_w_scales(1)
-        load_rows(u_raw[0], up[:, u_cols[0]])
-        load_w_words(2)
-        load_rows(u_raw[1], up[:, u_cols[1]])
+        load_rows(u_raw[OPEN], up[:, OPEN * GW : (OPEN + 1) * GW])
+        load_w_words(w_late, 2 * GW, N)
+        for c in (LATE, PARKED):
+            load_rows(u_raw[c], up[:, c * GW : (c + 1) * GW])
 
         def interleave(copy, dst, src, lo, hi):
             copy(
                 out=dst[:, lo:hi, :].rearrange("p (c i) t -> p c t i", i=4),
                 in_=src[:, :, lo:hi].rearrange("p t (c i) -> p c t i", i=4),
             )
-
-        def interleave_both(dst, src, split, width):
-            interleave(nc.vector.tensor_copy, dst, src, 0, split)
-            interleave(nc.scalar.copy, dst, src, split, width)
 
         def permute(copy, g, lo, hi):
             for t in (0, 2):
@@ -126,137 +113,137 @@ def tile_mix_lowrank_fm_bias_kernel(tc, x, w4_words, w4_scales, down, up, b, out
                     in_=d_raw[g][:, :, 4 * lo : 4 * hi].rearrange("p j (m t) -> p m j t", t=4)[:, :, :, t : t + 2],
                 )
 
-        def permute_both(g):
-            permute(nc.vector.tensor_copy, g, 0, DOWN_SPLIT)
-            permute(nc.scalar.copy, g, DOWN_SPLIT, P)
-
         def quantize(codes, scales, grouped):
             nc.vector.quantize_mx(out=codes.bitcast(E4M3X4), scales=scales, in_=grouped)
 
-        def quantize_rows(codes, scales, grouped):
-            quantize(codes[:], scales[:], grouped[:].rearrange("p w j -> p (w j)"))
+        def quantize_cols(codes, scales, grouped, lo, hi):
+            quantize(codes[:, lo:hi], scales[:, lo:hi], grouped[:, lo:hi, :].rearrange("p w j -> p (w j)"))
 
-        def w4_pass(i, acc, g):
-            c, m = i * P // WL, i * P % WL
-            d, n = (0, i * P) if i * P < W_COLS[0] else (1, i * P - W_COLS[0])
+        def w4_pass(i, g, stop):
+            words, m = (w_early, i * P) if i < 2 * GROUP else (w_late, (i - 2 * GROUP) * P)
             nc.tensor.matmul_mx(
-                out=acc,
-                lhsT=w_words[c][:, g, 2 * m : 2 * (m + P)].bitcast(E2M1X4),
-                lhsT_scale=w_scales[d][:, g, n : n + P],
+                out=acc[i][:],
+                lhsT=words[:, g, 2 * m : 2 * (m + P)].bitcast(E2M1X4),
+                lhsT_scale=w_scales[:, g, i * P : (i + 1) * P],
                 rhs=x_codes[g][:].bitcast(E4M3X4),
                 rhs_scale=x_scales[g][:],
                 start=(g == 0),
-                stop=False,
+                stop=stop,
             )
 
-        def up_pass(i, acc):
-            c, m = i * P // UL, i * P % UL
+        def up_pass(i, start):
+            c, m = i // GROUP, i % GROUP * P
             nc.tensor.matmul_mx(
-                out=acc,
+                out=acc[i][:],
                 lhsT=u_codes[c][:, m : m + P].bitcast(E4M3X4),
                 lhsT_scale=u_scales[c][:, m : m + P],
                 rhs=h_codes[:].bitcast(E4M3X4),
                 rhs_scale=h_scales[:],
-                start=False,
+                start=start,
                 stop=True,
             )
 
-        def h_pass(j, acc, g):
+        def h_pass(g, j, q):
             cols = slice(j * P, (j + 1) * P)
+            ts = slice(q * TQ, (q + 1) * TQ)
             nc.tensor.matmul_mx(
-                out=acc[:],
+                out=h_acc[q][:, j * TQ : (j + 1) * TQ],
                 lhsT=d_codes[g][:, cols].bitcast(E4M3X4),
                 lhsT_scale=d_scales[g][:, cols],
-                rhs=x_codes[g][:].bitcast(E4M3X4),
-                rhs_scale=x_scales[g][:],
-                start=(g == 0),
-                stop=(g == PASSES - 1),
+                rhs=x_codes[g][:, ts].bitcast(E4M3X4),
+                rhs_scale=x_scales[g][:, ts],
+                start=(g == 0 and j == 0),
+                stop=(g == PASSES - 1 and j == PACK - 1),
             )
 
-        def finish(i, acc, on_vector, ts=slice(0, T)):
-            bias = b_cols[:, i : i + 1]
-            if on_vector:
-                nc.vector.tensor_scalar(out=y_sb[i][:, ts], in0=acc, scalar1=bias, scalar2=None, op0=ADD)
-            else:
-                nc.scalar.activation(out=y_sb[i][:, ts], in_=acc, func=IDENTITY, bias=bias)
-            nc.sync.dma_start(out=out[i * P : (i + 1) * P, ts], in_=y_sb[i][:, ts])
+        def add_bias(i):
+            nc.scalar.activation(out=y_sb[i][:], in_=acc[i][:], func=IDENTITY, bias=b_cols[:, i : i + 1])
+
+        def store(i):
+            nc.sync.dma_start(out=out[i * P : (i + 1) * P, :], in_=y_sb[i][:])
+
+        def make_up(c):
+            interleave(nc.vector.tensor_copy, u_bf[c], u_raw[c], 0, GW)
+            quantize_cols(u_codes[c], u_scales[c], u_bf[c], 0, GW)
+
+        def tiles(c):
+            return range(c * GROUP, (c + 1) * GROUP)
 
         nc.scalar.activation(out=warm[:], in_=warm[:], func=IDENTITY)
         b_psum = bank(7, "b_psum")
         nc.tensor.transpose(b_psum[:, 0:P], b_rows[:], ident[:])
 
         acc = {}
-        h_acc = [bank(j, f"h{j}") for j in range(PACK)]
 
         for g in range(PASSES):
-            interleave_both(x_bf[g], x_raw[g], X_SPLIT, T)
+            interleave(nc.vector.tensor_copy, x_bf[g], x_raw[g], 0, X_SPLIT)
+            interleave(nc.scalar.copy, x_bf[g], x_raw[g], X_SPLIT, T)
             if g == 0:
                 nc.scalar.copy(out=b_cols[:], in_=b_psum[:, 0:N_TILES])
-                for i in range(4):
-                    acc[i] = bank(4 + i, f"y{i}")
-            quantize_rows(x_codes[g], x_scales[g], x_bf[g])
-            for i in range(4):
-                w4_pass(i, acc[i][:], g)
-            permute_both(g)
+                for i in range(2 * GROUP):
+                    acc[i] = bank(i, f"y{i}")
+            quantize_cols(x_codes[g], x_scales[g], x_bf[g], 0, T)
+            for i in range(2 * GROUP):
+                w4_pass(i, g, g == PASSES - 1 and i < GROUP)
+        for i in tiles(PARKED):
+            add_bias(i)
+
+        h_acc = [bank(q, f"h{q}") for q in range(PACK)]
+        for g in range(PASSES):
+            if g == 0:
+                permute(nc.vector.tensor_copy, g, 0, P)
+            else:
+                permute(nc.vector.tensor_copy, g, 0, DOWN_SPLIT)
+                permute(nc.scalar.copy, g, DOWN_SPLIT, P)
             if g < PASSES - 1:
                 quantize(d_codes[g][:], d_scales[g][:], d_bf[g][:].rearrange("p t m j -> p (t m j)"))
             else:
                 for j in range(PACK):
                     cols = slice(j * P, (j + 1) * P)
                     quantize(d_codes[g][:, cols], d_scales[g][:, cols], d_bf[g][:, j, :, :].rearrange("p m j -> p (m j)"))
-            for j in range(PACK):
-                h_pass(j, h_acc[j], g)
+            for js in ((0,), (1,), (2, 3)):
+                for q in range(PACK):
+                    for j in js:
+                        h_pass(g, j, q)
 
-        for j in range(PACK):
-            copy = nc.vector.tensor_copy if j % 2 else nc.scalar.copy
-            copy(out=h_sb[:, j, :], in_=h_acc[j][:])
-        interleave_both(h_bf, h_sb, H_SPLIT, T)
-        quantize_rows(h_codes, h_scales, h_bf)
+        def empty_h(copy, q):
+            copy(out=h_bf[:, q * TQ : (q + 1) * TQ, :], in_=h_acc[q][:].rearrange("p (j n) -> p n j", j=PACK))
 
-        def quantize_up(c, lo, hi):
-            quantize(u_codes[c][:, lo:hi], u_scales[c][:, lo:hi], u_bf[c][:, lo:hi, :].rearrange("p w j -> p (w j)"))
+        interleave(nc.vector.tensor_copy, u_bf[OPEN], u_raw[OPEN], 0, UP_SPLIT)
+        interleave(nc.scalar.copy, u_bf[OPEN], u_raw[OPEN], UP_SPLIT, GW)
+        empty_h(nc.scalar.copy, 0)
+        empty_h(nc.vector.tensor_copy, 1)
+        empty_h(nc.scalar.copy, 2)
+        empty_h(nc.scalar.copy, 3)
+        quantize_cols(u_codes[OPEN], u_scales[OPEN], u_bf[OPEN], 0, GW)
+        quantize_cols(h_codes, h_scales, h_bf, 0, T // 2)
+        quantize_cols(h_codes, h_scales, h_bf, T // 2, T)
 
-        def make_up(c):
-            interleave(nc.scalar.copy, u_bf[c], u_raw[c], UP_SPLIT, 512)
-            interleave(nc.vector.tensor_copy, u_bf[c], u_raw[c], 0, UP_SPLIT)
-            interleave(nc.scalar.copy, u_bf[c], u_raw[c], 640, UL)
-            interleave(nc.vector.tensor_copy, u_bf[c], u_raw[c], 512, 640)
-            quantize_up(c, 0, 512)
-            quantize_up(c, 512, UL)
-
-        def w4_tile(i):
-            acc[i] = bank(i - 4, f"y{i}")
+        def late_w4(i):
+            acc[i] = bank(i - 2 * GROUP, f"y{i}")
             for g in range(PASSES):
-                w4_pass(i, acc[i][:], g)
+                w4_pass(i, g, False)
 
-        def up_tile(i):
-            up_pass(i, acc[i][:])
+        def close(i):
+            up_pass(i, False)
+            add_bias(i)
+            store(i)
 
-        def out_tile(i, on_vector):
-            finish(i, acc[i][:], on_vector)
-
-        make_up(0)
-        for i in (4, 5, 6, 7):
-            w4_tile(i)
-        for i in range(6):
-            up_tile(i)
-        out_tile(0, False)
-        out_tile(1, True)
-        out_tile(2, False)
-        out_tile(3, True)
-        out_tile(4, False)
-        out_tile(5, True)
-        for i in (8, 9, 10):
-            w4_tile(i)
-        make_up(1)
-        for i in (6, 7, 8, 9, 10):
-            up_tile(i)
-        out_tile(6, False)
-        out_tile(7, True)
-        out_tile(8, False)
-        out_tile(9, True)
-        out_tile(10, False)
-        w4_tile(11)
-        up_tile(11)
-        finish(11, acc[11][:, 0 : T // 2], True, slice(0, T // 2))
-        finish(11, acc[11][:, T // 2 : T], True, slice(T // 2, T))
+        late = list(tiles(LATE))
+        late_w4(late[0])
+        late_w4(late[1])
+        make_up(LATE)
+        for i in tiles(OPEN):
+            close(i)
+        late_w4(late[2])
+        close(late[0])
+        close(late[1])
+        late_w4(late[3])
+        close(late[2])
+        close(late[3])
+        make_up(PARKED)
+        for i in tiles(PARKED):
+            acc[i] = bank(GROUP + i, f"z{i}")
+            up_pass(i, True)
+            nc.vector.tensor_tensor(out=y_sb[i][:], in0=acc[i][:], in1=y_sb[i][:], op=ADD)
+            store(i)

@@ -28,7 +28,7 @@ TQ = T // PACK
 
 X_SPLIT = 352
 DOWN_SPLIT = 88
-UP_SPLIT = 384
+PARKED_SHARE = 96
 
 
 def tile_mix_lowrank_fm_bias_kernel(tc, x, w4_words, w4_scales, down, up, b, out):
@@ -58,7 +58,8 @@ def tile_mix_lowrank_fm_bias_kernel(tc, x, w4_words, w4_scales, down, up, b, out
         u_scales = [sbuf(f"u_scales{c}", [P, GW], U8) for c in range(3)]
         w_early = sbuf("w_early", [P, PASSES, 2 * 2 * GW], U8)
         w_late = sbuf("w_late", [P, PASSES, 2 * GW], U8)
-        w_scales = sbuf("w_scales", [P, PASSES, N], U8)
+        s_early = sbuf("s_early", [P, PASSES, 2 * GW], U8)
+        s_late = sbuf("s_late", [P, PASSES, GW], U8)
         h_bf = sbuf("h_bf", [P, T, PACK], BF16)
         h_codes = sbuf("h_codes", [P, T], U32)
         h_scales = sbuf("h_scales", [P, T], U8)
@@ -69,8 +70,9 @@ def tile_mix_lowrank_fm_bias_kernel(tc, x, w4_words, w4_scales, down, up, b, out
         y_sb = [sbuf(f"y_sb{i}", [P, T], F32) for i in range(N_TILES)]
 
         nc.vector.memset(b_rows[:], 0.0)
-        nc.vector.memset(w_scales[:].rearrange("p g n -> p (g n)").bitcast(I32), 0)
+        nc.vector.memset(s_early[:].rearrange("p g n -> p (g n)").bitcast(I32), 0)
         nc.vector.memset(warm[:], 0.0)
+        nc.vector.memset(s_late[:].rearrange("p g n -> p (g n)").bitcast(I32), 0)
         make_identity(nc, ident[:])
 
         def load_rows(tile, rows):
@@ -79,23 +81,24 @@ def tile_mix_lowrank_fm_bias_kernel(tc, x, w4_words, w4_scales, down, up, b, out
         def load_w_words(tile, lo, hi):
             nc.sync.dma_start(out=tile[:], in_=w4_words[:, :, 2 * lo : 2 * hi].rearrange("g p n -> p g n"))
 
-        def load_w_scales():
+        def load_w_scales(tile, lo, hi):
             for r in range(4):
                 nc.sync.dma_start(
-                    out=w_scales[r:P:32, :, :].bitcast(I32),
-                    in_=w4_scales[:, r:16:4, :].rearrange("g q n -> q g n").bitcast(I32),
+                    out=tile[r:P:32, :, :].bitcast(I32),
+                    in_=w4_scales[:, r:16:4, lo:hi].rearrange("g q n -> q g n").bitcast(I32),
                 )
 
         k_rows = [slice(g * K_PASS, (g + 1) * K_PASS) for g in range(PASSES)]
         load_rows(x_raw[0], x[k_rows[0], :])
         nc.scalar.dma_start(out=b_rows[0:N_TILES, :], in_=b.rearrange("(c p) -> c p", p=P))
-        load_w_scales()
+        load_w_scales(s_early, 0, 2 * GW)
         load_w_words(w_early, 0, 2 * GW)
         for g in range(1, PASSES):
             load_rows(x_raw[g], x[k_rows[g], :])
         for g in range(PASSES):
             load_rows(d_raw[g], down[k_rows[g], :])
         load_rows(u_raw[OPEN], up[:, OPEN * GW : (OPEN + 1) * GW])
+        load_w_scales(s_late, 2 * GW, N)
         load_w_words(w_late, 2 * GW, N)
         for c in (LATE, PARKED):
             load_rows(u_raw[c], up[:, c * GW : (c + 1) * GW])
@@ -120,11 +123,11 @@ def tile_mix_lowrank_fm_bias_kernel(tc, x, w4_words, w4_scales, down, up, b, out
             quantize(codes[:, lo:hi], scales[:, lo:hi], grouped[:, lo:hi, :].rearrange("p w j -> p (w j)"))
 
         def w4_pass(i, g, stop):
-            words, m = (w_early, i * P) if i < 2 * GROUP else (w_late, (i - 2 * GROUP) * P)
+            words, scales, m = (w_early, s_early, i * P) if i < 2 * GROUP else (w_late, s_late, (i - 2 * GROUP) * P)
             nc.tensor.matmul_mx(
                 out=acc[i][:],
                 lhsT=words[:, g, 2 * m : 2 * (m + P)].bitcast(E2M1X4),
-                lhsT_scale=w_scales[:, g, i * P : (i + 1) * P],
+                lhsT_scale=scales[:, g, m : m + P],
                 rhs=x_codes[g][:].bitcast(E4M3X4),
                 rhs_scale=x_scales[g][:],
                 start=(g == 0),
@@ -162,9 +165,13 @@ def tile_mix_lowrank_fm_bias_kernel(tc, x, w4_words, w4_scales, down, up, b, out
         def store(i):
             nc.sync.dma_start(out=out[i * P : (i + 1) * P, :], in_=y_sb[i][:])
 
-        def make_up(c):
-            interleave(nc.vector.tensor_copy, u_bf[c], u_raw[c], 0, GW)
-            quantize_cols(u_codes[c], u_scales[c], u_bf[c], 0, GW)
+        def make_up(c, split):
+            interleave(nc.vector.tensor_copy, u_bf[c], u_raw[c], 0, GW // 2)
+            interleave(nc.vector.tensor_copy, u_bf[c], u_raw[c], GW // 2, split)
+            if split < GW:
+                interleave(nc.scalar.copy, u_bf[c], u_raw[c], split, GW)
+            quantize_cols(u_codes[c], u_scales[c], u_bf[c], 0, GW // 2)
+            quantize_cols(u_codes[c], u_scales[c], u_bf[c], GW // 2, GW)
 
         def tiles(c):
             return range(c * GROUP, (c + 1) * GROUP)
@@ -209,19 +216,21 @@ def tile_mix_lowrank_fm_bias_kernel(tc, x, w4_words, w4_scales, down, up, b, out
         def empty_h(copy, q):
             copy(out=h_bf[:, q * TQ : (q + 1) * TQ, :], in_=h_acc[q][:].rearrange("p (j n) -> p n j", j=PACK))
 
-        interleave(nc.vector.tensor_copy, u_bf[OPEN], u_raw[OPEN], 0, UP_SPLIT)
-        interleave(nc.scalar.copy, u_bf[OPEN], u_raw[OPEN], UP_SPLIT, GW)
+        interleave(nc.vector.tensor_copy, u_bf[OPEN], u_raw[OPEN], 0, GW // 2)
         empty_h(nc.scalar.copy, 0)
         empty_h(nc.vector.tensor_copy, 1)
         empty_h(nc.scalar.copy, 2)
         empty_h(nc.scalar.copy, 3)
-        quantize_cols(u_codes[OPEN], u_scales[OPEN], u_bf[OPEN], 0, GW)
+        quantize_cols(u_codes[OPEN], u_scales[OPEN], u_bf[OPEN], 0, GW // 2)
         quantize_cols(h_codes, h_scales, h_bf, 0, T // 2)
         quantize_cols(h_codes, h_scales, h_bf, T // 2, T)
+        interleave(nc.vector.tensor_copy, u_bf[OPEN], u_raw[OPEN], GW // 2, GW)
+        quantize_cols(u_codes[OPEN], u_scales[OPEN], u_bf[OPEN], GW // 2, GW)
 
-        def late_w4(i):
-            acc[i] = bank(i - 2 * GROUP, f"y{i}")
-            for g in range(PASSES):
+        def late_w4(i, passes):
+            if passes[0] == 0:
+                acc[i] = bank(i - 2 * GROUP, f"y{i}")
+            for g in passes:
                 w4_pass(i, g, False)
 
         def close(i):
@@ -229,21 +238,29 @@ def tile_mix_lowrank_fm_bias_kernel(tc, x, w4_words, w4_scales, down, up, b, out
             add_bias(i)
             store(i)
 
-        late = list(tiles(LATE))
-        late_w4(late[0])
-        late_w4(late[1])
-        make_up(LATE)
-        for i in tiles(OPEN):
-            close(i)
-        late_w4(late[2])
-        close(late[0])
-        close(late[1])
-        late_w4(late[3])
-        close(late[2])
-        close(late[3])
-        make_up(PARKED)
-        for i in tiles(PARKED):
+        def close_parked(i):
             acc[i] = bank(GROUP + i, f"z{i}")
             up_pass(i, True)
             nc.vector.tensor_tensor(out=y_sb[i][:], in0=acc[i][:], in1=y_sb[i][:], op=ADD)
             store(i)
+
+        late = list(tiles(LATE))
+        late_w4(late[0], (0, 1, 2, 3))
+        make_up(LATE, GW)
+        close(GROUP)
+        close(GROUP + 1)
+        late_w4(late[1], (0, 1))
+        close(GROUP + 2)
+        close(GROUP + 3)
+        late_w4(late[1], (2, 3))
+        make_up(PARKED, GW - PARKED_SHARE)
+        late_w4(late[2], (0, 1, 2, 3))
+        for i in late[:3]:
+            close(i)
+        late_w4(late[3], (0, 1, 2))
+        close_parked(0)
+        close_parked(1)
+        late_w4(late[3], (3,))
+        close(late[3])
+        close_parked(2)
+        close_parked(3)

@@ -58,7 +58,7 @@ def tile_mix_lowrank_fm_bias_kernel(tc, x, w4_words, w4_scales, down, up, b, out
         u_scales = [sbuf(f"u_scales{c}", [P, GW], U8) for c in range(3)]
         w_early = sbuf("w_early", [P, PASSES, 2 * 2 * GW], U8)
         w_late = sbuf("w_late", [P, PASSES, 2 * GW], U8)
-        s_early = sbuf("s_early", [P, PASSES, 2 * GW], U8)
+        s_early = [sbuf(f"s_early{h}", [P, 2, 2 * GW], U8) for h in range(2)]
         s_late = sbuf("s_late", [P, PASSES, GW], U8)
         h_bf = sbuf("h_bf", [P, T, PACK], BF16)
         h_codes = sbuf("h_codes", [P, T], U32)
@@ -70,7 +70,8 @@ def tile_mix_lowrank_fm_bias_kernel(tc, x, w4_words, w4_scales, down, up, b, out
         y_sb = [sbuf(f"y_sb{i}", [P, T], F32) for i in range(N_TILES)]
 
         nc.vector.memset(b_rows[:], 0.0)
-        nc.vector.memset(s_early[:].rearrange("p g n -> p (g n)").bitcast(I32), 0)
+        for h in (1, 0):
+            nc.vector.memset(s_early[h][:].rearrange("p g n -> p (g n)").bitcast(I32), 0)
         nc.vector.memset(warm[:], 0.0)
         nc.vector.memset(s_late[:].rearrange("p g n -> p (g n)").bitcast(I32), 0)
         make_identity(nc, ident[:])
@@ -81,24 +82,25 @@ def tile_mix_lowrank_fm_bias_kernel(tc, x, w4_words, w4_scales, down, up, b, out
         def load_w_words(tile, lo, hi):
             nc.sync.dma_start(out=tile[:], in_=w4_words[:, :, 2 * lo : 2 * hi].rearrange("g p n -> p g n"))
 
-        def load_w_scales(tile, lo, hi):
+        def load_w_scales(queue, tile, passes, lo, hi):
             for r in range(4):
-                nc.sync.dma_start(
+                queue.dma_start(
                     out=tile[r:P:32, :, :].bitcast(I32),
-                    in_=w4_scales[:, r:16:4, lo:hi].rearrange("g q n -> q g n").bitcast(I32),
+                    in_=w4_scales[passes, r:16:4, lo:hi].rearrange("g q n -> q g n").bitcast(I32),
                 )
 
         k_rows = [slice(g * K_PASS, (g + 1) * K_PASS) for g in range(PASSES)]
         load_rows(x_raw[0], x[k_rows[0], :])
         nc.scalar.dma_start(out=b_rows[0:N_TILES, :], in_=b.rearrange("(c p) -> c p", p=P))
-        load_w_scales(s_early, 0, 2 * GW)
+        load_w_scales(nc.sync, s_early[0], slice(0, 2), 0, 2 * GW)
+        load_w_scales(nc.gpsimd, s_early[1], slice(2, 4), 0, 2 * GW)
+        load_w_scales(nc.gpsimd, s_late, slice(0, 4), 2 * GW, N)
         load_w_words(w_early, 0, 2 * GW)
         for g in range(1, PASSES):
             load_rows(x_raw[g], x[k_rows[g], :])
         for g in range(PASSES):
             load_rows(d_raw[g], down[k_rows[g], :])
         load_rows(u_raw[OPEN], up[:, OPEN * GW : (OPEN + 1) * GW])
-        load_w_scales(s_late, 2 * GW, N)
         load_w_words(w_late, 2 * GW, N)
         for c in (LATE, PARKED):
             load_rows(u_raw[c], up[:, c * GW : (c + 1) * GW])
@@ -123,11 +125,11 @@ def tile_mix_lowrank_fm_bias_kernel(tc, x, w4_words, w4_scales, down, up, b, out
             quantize(codes[:, lo:hi], scales[:, lo:hi], grouped[:, lo:hi, :].rearrange("p w j -> p (w j)"))
 
         def w4_pass(i, g, stop):
-            words, scales, m = (w_early, s_early, i * P) if i < 2 * GROUP else (w_late, s_late, (i - 2 * GROUP) * P)
+            words, scales, m = (w_early, s_early[g // 2][:, g % 2, :], i * P) if i < 2 * GROUP else (w_late, s_late[:, g, :], (i - 2 * GROUP) * P)
             nc.tensor.matmul_mx(
                 out=acc[i][:],
                 lhsT=words[:, g, 2 * m : 2 * (m + P)].bitcast(E2M1X4),
-                lhsT_scale=scales[:, g, m : m + P],
+                lhsT_scale=scales[:, m : m + P],
                 rhs=x_codes[g][:].bitcast(E4M3X4),
                 rhs_scale=x_scales[g][:],
                 start=(g == 0),
@@ -221,10 +223,10 @@ def tile_mix_lowrank_fm_bias_kernel(tc, x, w4_words, w4_scales, down, up, b, out
         empty_h(nc.vector.tensor_copy, 1)
         empty_h(nc.scalar.copy, 2)
         empty_h(nc.scalar.copy, 3)
+        interleave(nc.scalar.copy, u_bf[OPEN], u_raw[OPEN], GW // 2, GW)
         quantize_cols(u_codes[OPEN], u_scales[OPEN], u_bf[OPEN], 0, GW // 2)
         quantize_cols(h_codes, h_scales, h_bf, 0, T // 2)
         quantize_cols(h_codes, h_scales, h_bf, T // 2, T)
-        interleave(nc.vector.tensor_copy, u_bf[OPEN], u_raw[OPEN], GW // 2, GW)
         quantize_cols(u_codes[OPEN], u_scales[OPEN], u_bf[OPEN], GW // 2, GW)
 
         def late_w4(i, passes):

@@ -24,11 +24,12 @@ N_TILES = N // P
 GROUP = 4
 GW = GROUP * P
 PARKED, OPEN, LATE = 0, 1, 2
+EARLY = 2 * GROUP
 TQ = T // PACK
 
 X_SPLIT = 352
 DOWN_SPLIT = 88
-PARKED_SHARE = 96
+PARKED_SHARE = 192
 
 
 def tile_mix_lowrank_fm_bias_kernel(tc, x, w4_words, w4_scales, down, up, b, out):
@@ -41,8 +42,8 @@ def tile_mix_lowrank_fm_bias_kernel(tc, x, w4_words, w4_scales, down, up, b, out
         def sbuf(name, shape, dtype):
             return keep.tile(shape, dtype, name=name, align_bytes=64)
 
-        def bank(i, name):
-            return psum.tile([P, T], F32, name=name, tag=f"bank{i}")
+        def bank(number, name):
+            return psum.tile([P, T], F32, name=name, tag=f"bank{number}")
 
         x_raw = [sbuf(f"x_raw{g}", [P, PACK, T], F32) for g in range(PASSES)]
         x_bf = [sbuf(f"x_bf{g}", [P, T, PACK], BF16) for g in range(PASSES)]
@@ -52,13 +53,13 @@ def tile_mix_lowrank_fm_bias_kernel(tc, x, w4_words, w4_scales, down, up, b, out
         d_bf = [sbuf(f"d_bf{g}", [P, PACK, P, PACK], BF16) for g in range(PASSES)]
         d_codes = [sbuf(f"d_codes{g}", [P, R], U32) for g in range(PASSES)]
         d_scales = [sbuf(f"d_scales{g}", [P, R], U8) for g in range(PASSES)]
-        u_raw = [sbuf(f"u_raw{c}", [P, PACK, GW], F32) for c in range(3)]
-        u_bf = [sbuf(f"u_bf{c}", [P, GW, PACK], BF16) for c in range(3)]
-        u_codes = [sbuf(f"u_codes{c}", [P, GW], U32) for c in range(3)]
-        u_scales = [sbuf(f"u_scales{c}", [P, GW], U8) for c in range(3)]
-        w_early = sbuf("w_early", [P, PASSES, 2 * 2 * GW], U8)
+        u_raw = [sbuf(f"u_raw{c}", [P, PACK, GW], F32) for c in (PARKED, OPEN, LATE)]
+        u_bf = [sbuf(f"u_bf{c}", [P, GW, PACK], BF16) for c in (PARKED, OPEN, LATE)]
+        u_codes = [sbuf(f"u_codes{c}", [P, GW], U32) for c in (PARKED, OPEN, LATE)]
+        u_scales = [sbuf(f"u_scales{c}", [P, GW], U8) for c in (PARKED, OPEN, LATE)]
+        w_early = sbuf("w_early", [P, PASSES, 2 * EARLY * P], U8)
         w_late = sbuf("w_late", [P, PASSES, 2 * GW], U8)
-        s_early = [sbuf(f"s_early{h}", [P, 2, 2 * GW], U8) for h in range(2)]
+        s_early = [sbuf(f"s_early{half}", [P, PASSES // 2, EARLY * P], U8) for half in range(2)]
         s_late = sbuf("s_late", [P, PASSES, GW], U8)
         h_bf = sbuf("h_bf", [P, T, PACK], BF16)
         h_codes = sbuf("h_codes", [P, T], U32)
@@ -66,14 +67,11 @@ def tile_mix_lowrank_fm_bias_kernel(tc, x, w4_words, w4_scales, down, up, b, out
         ident = sbuf("ident", [P, P], F32)
         b_rows = sbuf("b_rows", [P, P], F32)
         b_cols = sbuf("b_cols", [P, N_TILES], F32)
-        warm = sbuf("warm", [P, 1], F32)
         y_sb = [sbuf(f"y_sb{i}", [P, T], F32) for i in range(N_TILES)]
 
         nc.vector.memset(b_rows[:], 0.0)
-        for h in (1, 0):
-            nc.vector.memset(s_early[h][:].rearrange("p g n -> p (g n)").bitcast(I32), 0)
-        nc.vector.memset(warm[:], 0.0)
-        nc.vector.memset(s_late[:].rearrange("p g n -> p (g n)").bitcast(I32), 0)
+        for tile in (s_early[1], s_early[0], s_late):
+            nc.vector.memset(tile[:].rearrange("p g n -> p (g n)").bitcast(I32), 0)
         make_identity(nc, ident[:])
 
         def load_rows(tile, rows):
@@ -83,39 +81,38 @@ def tile_mix_lowrank_fm_bias_kernel(tc, x, w4_words, w4_scales, down, up, b, out
             nc.sync.dma_start(out=tile[:], in_=w4_words[:, :, 2 * lo : 2 * hi].rearrange("g p n -> p g n"))
 
         def load_w_scales(queue, tile, passes, lo, hi):
-            for r in range(4):
+            for s in range(4):
                 queue.dma_start(
-                    out=tile[r:P:32, :, :].bitcast(I32),
-                    in_=w4_scales[passes, r:16:4, lo:hi].rearrange("g q n -> q g n").bitcast(I32),
+                    out=tile[s:P:32, :, :].bitcast(I32),
+                    in_=w4_scales[passes, s:16:4, lo:hi].rearrange("g q n -> q g n").bitcast(I32),
                 )
 
         k_rows = [slice(g * K_PASS, (g + 1) * K_PASS) for g in range(PASSES)]
         load_rows(x_raw[0], x[k_rows[0], :])
         nc.scalar.dma_start(out=b_rows[0:N_TILES, :], in_=b.rearrange("(c p) -> c p", p=P))
-        load_w_scales(nc.sync, s_early[0], slice(0, 2), 0, 2 * GW)
-        load_w_scales(nc.gpsimd, s_early[1], slice(2, 4), 0, 2 * GW)
-        load_w_scales(nc.gpsimd, s_late, slice(0, 4), 2 * GW, N)
-        load_w_words(w_early, 0, 2 * GW)
+        load_w_scales(nc.sync, s_early[0], slice(0, PASSES // 2), 0, EARLY * P)
+        load_w_scales(nc.gpsimd, s_early[1], slice(PASSES // 2, PASSES), 0, EARLY * P)
+        load_w_scales(nc.gpsimd, s_late, slice(0, PASSES), EARLY * P, N)
+        load_w_words(w_early, 0, EARLY * P)
         for g in range(1, PASSES):
             load_rows(x_raw[g], x[k_rows[g], :])
         for g in range(PASSES):
             load_rows(d_raw[g], down[k_rows[g], :])
-        load_rows(u_raw[OPEN], up[:, OPEN * GW : (OPEN + 1) * GW])
-        load_w_words(w_late, 2 * GW, N)
-        for c in (LATE, PARKED):
+        load_w_words(w_late, EARLY * P, N)
+        for c in (OPEN, LATE, PARKED):
             load_rows(u_raw[c], up[:, c * GW : (c + 1) * GW])
 
         def interleave(copy, dst, src, lo, hi):
             copy(
-                out=dst[:, lo:hi, :].rearrange("p (c i) t -> p c t i", i=4),
-                in_=src[:, :, lo:hi].rearrange("p t (c i) -> p c t i", i=4),
+                out=dst[:, lo:hi, :].rearrange("p (c i) j -> p c j i", i=4),
+                in_=src[:, :, lo:hi].rearrange("p j (c i) -> p c j i", i=4),
             )
 
         def permute(copy, g, lo, hi):
-            for t in (0, 2):
+            for a in (0, 2):
                 copy(
-                    out=d_bf[g][:, t : t + 2, lo:hi, :].rearrange("p t m j -> p m j t"),
-                    in_=d_raw[g][:, :, 4 * lo : 4 * hi].rearrange("p j (m t) -> p m j t", t=4)[:, :, :, t : t + 2],
+                    out=d_bf[g][:, a : a + 2, lo:hi, :].rearrange("p a m j -> p m j a"),
+                    in_=d_raw[g][:, :, 4 * lo : 4 * hi].rearrange("p j (m a) -> p m j a", a=4)[:, :, :, a : a + 2],
                 )
 
         def quantize(codes, scales, grouped):
@@ -125,11 +122,14 @@ def tile_mix_lowrank_fm_bias_kernel(tc, x, w4_words, w4_scales, down, up, b, out
             quantize(codes[:, lo:hi], scales[:, lo:hi], grouped[:, lo:hi, :].rearrange("p w j -> p (w j)"))
 
         def w4_pass(i, g, stop):
-            words, scales, m = (w_early, s_early[g // 2][:, g % 2, :], i * P) if i < 2 * GROUP else (w_late, s_late[:, g, :], (i - 2 * GROUP) * P)
+            if i < EARLY:
+                words, scales, col = w_early, s_early[g // 2][:, g % 2, :], i * P
+            else:
+                words, scales, col = w_late, s_late[:, g, :], (i - EARLY) * P
             nc.tensor.matmul_mx(
                 out=acc[i][:],
-                lhsT=words[:, g, 2 * m : 2 * (m + P)].bitcast(E2M1X4),
-                lhsT_scale=scales[:, m : m + P],
+                lhsT=words[:, g, 2 * col : 2 * (col + P)].bitcast(E2M1X4),
+                lhsT_scale=scales[:, col : col + P],
                 rhs=x_codes[g][:].bitcast(E4M3X4),
                 rhs_scale=x_scales[g][:],
                 start=(g == 0),
@@ -137,28 +137,28 @@ def tile_mix_lowrank_fm_bias_kernel(tc, x, w4_words, w4_scales, down, up, b, out
             )
 
         def up_pass(i, start):
-            c, m = i // GROUP, i % GROUP * P
+            c, col = i // GROUP, i % GROUP * P
             nc.tensor.matmul_mx(
                 out=acc[i][:],
-                lhsT=u_codes[c][:, m : m + P].bitcast(E4M3X4),
-                lhsT_scale=u_scales[c][:, m : m + P],
+                lhsT=u_codes[c][:, col : col + P].bitcast(E4M3X4),
+                lhsT_scale=u_scales[c][:, col : col + P],
                 rhs=h_codes[:].bitcast(E4M3X4),
                 rhs_scale=h_scales[:],
                 start=start,
                 stop=True,
             )
 
-        def h_pass(g, j, q):
-            cols = slice(j * P, (j + 1) * P)
+        def h_pass(g, a, q):
+            cols = slice(a * P, (a + 1) * P)
             ts = slice(q * TQ, (q + 1) * TQ)
             nc.tensor.matmul_mx(
-                out=h_acc[q][:, j * TQ : (j + 1) * TQ],
+                out=h_acc[q][:, a * TQ : (a + 1) * TQ],
                 lhsT=d_codes[g][:, cols].bitcast(E4M3X4),
                 lhsT_scale=d_scales[g][:, cols],
                 rhs=x_codes[g][:, ts].bitcast(E4M3X4),
                 rhs_scale=x_scales[g][:, ts],
-                start=(g == 0 and j == 0),
-                stop=(g == PASSES - 1 and j == PACK - 1),
+                start=(g == 0 and a == 0),
+                stop=(g == PASSES - 1 and a == PACK - 1),
             )
 
         def add_bias(i):
@@ -176,24 +176,19 @@ def tile_mix_lowrank_fm_bias_kernel(tc, x, w4_words, w4_scales, down, up, b, out
             quantize_cols(u_codes[c], u_scales[c], u_bf[c], GW // 2, GW)
 
         def tiles(c):
-            return range(c * GROUP, (c + 1) * GROUP)
+            return list(range(c * GROUP, (c + 1) * GROUP))
 
-        nc.scalar.activation(out=warm[:], in_=warm[:], func=IDENTITY)
-        b_psum = bank(7, "b_psum")
+        b_psum = bank(EARLY - 1, "b_psum")
         nc.tensor.transpose(b_psum[:, 0:P], b_rows[:], ident[:])
+        nc.scalar.activation(out=b_cols[:], in_=b_psum[:, 0:N_TILES], func=IDENTITY)
 
-        acc = {}
-
+        acc = {i: bank(i, f"y{i}") for i in range(EARLY)}
         for g in range(PASSES):
             interleave(nc.vector.tensor_copy, x_bf[g], x_raw[g], 0, X_SPLIT)
             interleave(nc.scalar.copy, x_bf[g], x_raw[g], X_SPLIT, T)
-            if g == 0:
-                nc.scalar.copy(out=b_cols[:], in_=b_psum[:, 0:N_TILES])
-                for i in range(2 * GROUP):
-                    acc[i] = bank(i, f"y{i}")
             quantize_cols(x_codes[g], x_scales[g], x_bf[g], 0, T)
-            for i in range(2 * GROUP):
-                w4_pass(i, g, g == PASSES - 1 and i < GROUP)
+            for i in range(EARLY):
+                w4_pass(i, g, stop=(g == PASSES - 1 and i in tiles(PARKED)))
         for i in tiles(PARKED):
             add_bias(i)
 
@@ -205,64 +200,55 @@ def tile_mix_lowrank_fm_bias_kernel(tc, x, w4_words, w4_scales, down, up, b, out
                 permute(nc.vector.tensor_copy, g, 0, DOWN_SPLIT)
                 permute(nc.scalar.copy, g, DOWN_SPLIT, P)
             if g < PASSES - 1:
-                quantize(d_codes[g][:], d_scales[g][:], d_bf[g][:].rearrange("p t m j -> p (t m j)"))
+                quantize(d_codes[g][:], d_scales[g][:], d_bf[g][:].rearrange("p a m j -> p (a m j)"))
             else:
-                for j in range(PACK):
-                    cols = slice(j * P, (j + 1) * P)
-                    quantize(d_codes[g][:, cols], d_scales[g][:, cols], d_bf[g][:, j, :, :].rearrange("p m j -> p (m j)"))
-            for js in ((0,), (1,), (2, 3)):
+                for a in range(PACK):
+                    cols = slice(a * P, (a + 1) * P)
+                    quantize(d_codes[g][:, cols], d_scales[g][:, cols], d_bf[g][:, a, :, :].rearrange("p m j -> p (m j)"))
+            for parts in ((0,), (1,), (2, 3)):
                 for q in range(PACK):
-                    for j in js:
-                        h_pass(g, j, q)
+                    for a in parts:
+                        h_pass(g, a, q)
 
-        def empty_h(copy, q):
-            copy(out=h_bf[:, q * TQ : (q + 1) * TQ, :], in_=h_acc[q][:].rearrange("p (j n) -> p n j", j=PACK))
+        for q in range(PACK):
+            copy = nc.vector.tensor_copy if q % 2 else nc.scalar.copy
+            copy(out=h_bf[:, q * TQ : (q + 1) * TQ, :], in_=h_acc[q][:].rearrange("p (a n) -> p n a", a=PACK))
 
-        interleave(nc.vector.tensor_copy, u_bf[OPEN], u_raw[OPEN], 0, GW // 2)
-        empty_h(nc.scalar.copy, 0)
-        empty_h(nc.vector.tensor_copy, 1)
-        empty_h(nc.scalar.copy, 2)
-        empty_h(nc.scalar.copy, 3)
         interleave(nc.scalar.copy, u_bf[OPEN], u_raw[OPEN], GW // 2, GW)
-        quantize_cols(u_codes[OPEN], u_scales[OPEN], u_bf[OPEN], 0, GW // 2)
         quantize_cols(h_codes, h_scales, h_bf, 0, T // 2)
+        interleave(nc.vector.tensor_copy, u_bf[OPEN], u_raw[OPEN], 0, GW // 2)
         quantize_cols(h_codes, h_scales, h_bf, T // 2, T)
+        quantize_cols(u_codes[OPEN], u_scales[OPEN], u_bf[OPEN], 0, GW // 2)
         quantize_cols(u_codes[OPEN], u_scales[OPEN], u_bf[OPEN], GW // 2, GW)
 
-        def late_w4(i, passes):
-            if passes[0] == 0:
-                acc[i] = bank(i - 2 * GROUP, f"y{i}")
-            for g in passes:
-                w4_pass(i, g, False)
+        def late_w4(i):
+            acc[i] = bank(i - EARLY, f"y{i}")
+            for g in range(PASSES):
+                w4_pass(i, g, stop=False)
 
         def close(i):
-            up_pass(i, False)
+            up_pass(i, start=False)
             add_bias(i)
             store(i)
 
         def close_parked(i):
             acc[i] = bank(GROUP + i, f"z{i}")
-            up_pass(i, True)
+            up_pass(i, start=True)
             nc.vector.tensor_tensor(out=y_sb[i][:], in0=acc[i][:], in1=y_sb[i][:], op=ADD)
             store(i)
 
-        late = list(tiles(LATE))
-        late_w4(late[0], (0, 1, 2, 3))
+        late, parked = tiles(LATE), tiles(PARKED)
+        late_w4(late[0])
+        late_w4(late[1])
         make_up(LATE, GW)
-        close(GROUP)
-        close(GROUP + 1)
-        late_w4(late[1], (0, 1))
-        close(GROUP + 2)
-        close(GROUP + 3)
-        late_w4(late[1], (2, 3))
+        for i in tiles(OPEN):
+            close(i)
         make_up(PARKED, GW - PARKED_SHARE)
-        late_w4(late[2], (0, 1, 2, 3))
+        late_w4(late[2])
         for i in late[:3]:
             close(i)
-        late_w4(late[3], (0, 1, 2))
-        close_parked(0)
-        close_parked(1)
-        late_w4(late[3], (3,))
+        late_w4(late[3])
+        close_parked(parked[0])
         close(late[3])
-        close_parked(2)
-        close_parked(3)
+        for i in parked[1:]:
+            close_parked(i)

@@ -27,9 +27,12 @@ PARKED, OPEN, LATE = 0, 1, 2
 EARLY = 2 * GROUP
 TQ = T // PACK
 
+HALF = GW // 2
+PAIR = 2
+
 X_SPLIT = 352
-DOWN_SPLIT = 88
-PARKED_SHARE = 192
+DOWN_SPLIT = 48
+LEAD = 5
 
 
 def tile_mix_lowrank_fm_bias_kernel(tc, x, w4_words, w4_scales, down, up, b, out):
@@ -98,9 +101,10 @@ def tile_mix_lowrank_fm_bias_kernel(tc, x, w4_words, w4_scales, down, up, b, out
             load_rows(x_raw[g], x[k_rows[g], :])
         for g in range(PASSES):
             load_rows(d_raw[g], down[k_rows[g], :])
-        load_w_words(w_late, EARLY * P, N)
-        for c in (OPEN, LATE, PARKED):
+        for c in (OPEN, PARKED, LATE):
             load_rows(u_raw[c], up[:, c * GW : (c + 1) * GW])
+            if c == OPEN:
+                load_w_words(w_late, EARLY * P, N)
 
         def interleave(copy, dst, src, lo, hi):
             copy(
@@ -108,12 +112,11 @@ def tile_mix_lowrank_fm_bias_kernel(tc, x, w4_words, w4_scales, down, up, b, out
                 in_=src[:, :, lo:hi].rearrange("p j (c i) -> p c j i", i=4),
             )
 
-        def permute(copy, g, lo, hi):
-            for a in (0, 2):
-                copy(
-                    out=d_bf[g][:, a : a + 2, lo:hi, :].rearrange("p a m j -> p m j a"),
-                    in_=d_raw[g][:, :, 4 * lo : 4 * hi].rearrange("p j (m a) -> p m j a", a=4)[:, :, :, a : a + 2],
-                )
+        def permute(copy, g, a, lo, hi):
+            copy(
+                out=d_bf[g][:, a : a + 2, lo:hi, :].rearrange("p a m j -> p m j a"),
+                in_=d_raw[g][:, :, 4 * lo : 4 * hi].rearrange("p j (m a) -> p m j a", a=4)[:, :, :, a : a + 2],
+            )
 
         def quantize(codes, scales, grouped):
             nc.vector.quantize_mx(out=codes.bitcast(E4M3X4), scales=scales, in_=grouped)
@@ -161,19 +164,20 @@ def tile_mix_lowrank_fm_bias_kernel(tc, x, w4_words, w4_scales, down, up, b, out
                 stop=(g == PASSES - 1 and a == PACK - 1),
             )
 
-        def add_bias(i):
+        def add_bias_scalar(i):
             nc.scalar.activation(out=y_sb[i][:], in_=acc[i][:], func=IDENTITY, bias=b_cols[:, i : i + 1])
+
+        def add_bias_vector(i):
+            nc.vector.tensor_scalar_add(out=y_sb[i][:], in0=acc[i][:], scalar1=b_cols[:, i : i + 1])
 
         def store(i):
             nc.sync.dma_start(out=out[i * P : (i + 1) * P, :], in_=y_sb[i][:])
 
-        def make_up(c, split):
-            interleave(nc.vector.tensor_copy, u_bf[c], u_raw[c], 0, GW // 2)
-            interleave(nc.vector.tensor_copy, u_bf[c], u_raw[c], GW // 2, split)
-            if split < GW:
-                interleave(nc.scalar.copy, u_bf[c], u_raw[c], split, GW)
-            quantize_cols(u_codes[c], u_scales[c], u_bf[c], 0, GW // 2)
-            quantize_cols(u_codes[c], u_scales[c], u_bf[c], GW // 2, GW)
+        def cast_up(copy, c, lo, hi):
+            interleave(copy, u_bf[c], u_raw[c], lo, hi)
+
+        def quantize_up(c, lo):
+            quantize_cols(u_codes[c], u_scales[c], u_bf[c], lo, lo + HALF)
 
         def tiles(c):
             return list(range(c * GROUP, (c + 1) * GROUP))
@@ -187,18 +191,27 @@ def tile_mix_lowrank_fm_bias_kernel(tc, x, w4_words, w4_scales, down, up, b, out
             interleave(nc.vector.tensor_copy, x_bf[g], x_raw[g], 0, X_SPLIT)
             interleave(nc.scalar.copy, x_bf[g], x_raw[g], X_SPLIT, T)
             quantize_cols(x_codes[g], x_scales[g], x_bf[g], 0, T)
-            for i in range(EARLY):
-                w4_pass(i, g, stop=(g == PASSES - 1 and i in tiles(PARKED)))
+            for i in tiles(PARKED):
+                w4_pass(i, g, stop=(g == PASSES - 1))
+            if g < PASSES // 2:
+                for i in tiles(OPEN):
+                    w4_pass(i, g, stop=False)
+        for g in range(PASSES // 2, PASSES):
+            for i in tiles(OPEN):
+                w4_pass(i, g, stop=False)
         for i in tiles(PARKED):
-            add_bias(i)
+            add_bias_scalar(i)
 
         h_acc = [bank(q, f"h{q}") for q in range(PACK)]
         for g in range(PASSES):
-            if g == 0:
-                permute(nc.vector.tensor_copy, g, 0, P)
+            permute(nc.vector.tensor_copy, g, 0, 0, P)
+            if g < PASSES // 2:
+                permute(nc.vector.tensor_copy, g, 2, 0, P)
+            elif g < PASSES - 1:
+                permute(nc.vector.tensor_copy, g, 2, 0, DOWN_SPLIT)
+                permute(nc.scalar.copy, g, 2, DOWN_SPLIT, P)
             else:
-                permute(nc.vector.tensor_copy, g, 0, DOWN_SPLIT)
-                permute(nc.scalar.copy, g, DOWN_SPLIT, P)
+                permute(nc.scalar.copy, g, 2, 0, P)
             if g < PASSES - 1:
                 quantize(d_codes[g][:], d_scales[g][:], d_bf[g][:].rearrange("p a m j -> p (a m j)"))
             else:
@@ -210,23 +223,27 @@ def tile_mix_lowrank_fm_bias_kernel(tc, x, w4_words, w4_scales, down, up, b, out
                     for a in parts:
                         h_pass(g, a, q)
 
+        cast_up(nc.vector.tensor_copy, OPEN, 0, HALF)
         for q in range(PACK):
-            copy = nc.vector.tensor_copy if q % 2 else nc.scalar.copy
+            copy = nc.vector.tensor_copy if q == PACK - 1 else nc.scalar.copy
             copy(out=h_bf[:, q * TQ : (q + 1) * TQ, :], in_=h_acc[q][:].rearrange("p (a n) -> p n a", a=PACK))
-
-        interleave(nc.scalar.copy, u_bf[OPEN], u_raw[OPEN], GW // 2, GW)
+        quantize_up(OPEN, 0)
         quantize_cols(h_codes, h_scales, h_bf, 0, T // 2)
-        interleave(nc.vector.tensor_copy, u_bf[OPEN], u_raw[OPEN], 0, GW // 2)
         quantize_cols(h_codes, h_scales, h_bf, T // 2, T)
-        quantize_cols(u_codes[OPEN], u_scales[OPEN], u_bf[OPEN], 0, GW // 2)
-        quantize_cols(u_codes[OPEN], u_scales[OPEN], u_bf[OPEN], GW // 2, GW)
+        cast_up(nc.scalar.copy, OPEN, HALF, HALF + P)
+        cast_up(nc.vector.tensor_copy, OPEN, HALF + P, GW)
+        quantize_up(OPEN, HALF)
 
-        def late_w4(i):
-            acc[i] = bank(i - EARLY, f"y{i}")
-            for g in range(PASSES):
+        late_passes = [(i, g) for i in tiles(LATE) for g in range(PASSES)]
+
+        def late_w4(count):
+            for i, g in late_passes[:count]:
+                if g == 0:
+                    acc[i] = bank(i - EARLY, f"y{i}")
                 w4_pass(i, g, stop=False)
+                late_passes.remove((i, g))
 
-        def close(i):
+        def close(i, add_bias):
             up_pass(i, start=False)
             add_bias(i)
             store(i)
@@ -237,18 +254,26 @@ def tile_mix_lowrank_fm_bias_kernel(tc, x, w4_words, w4_scales, down, up, b, out
             nc.vector.tensor_tensor(out=y_sb[i][:], in0=acc[i][:], in1=y_sb[i][:], op=ADD)
             store(i)
 
-        late, parked = tiles(LATE), tiles(PARKED)
-        late_w4(late[0])
-        late_w4(late[1])
-        make_up(LATE, GW)
-        for i in tiles(OPEN):
-            close(i)
-        make_up(PARKED, GW - PARKED_SHARE)
-        late_w4(late[2])
-        for i in late[:3]:
-            close(i)
-        late_w4(late[3])
-        close_parked(parked[0])
-        close(late[3])
-        for i in parked[1:]:
-            close_parked(i)
+        def pairs(c):
+            return [tiles(c)[first : first + PAIR] for first in range(0, GROUP, PAIR)]
+
+        late_w4(LEAD)
+        for lo in (0, HALF):
+            cast_up(nc.vector.tensor_copy, PARKED, lo, lo + HALF)
+        for lo in (0, HALF):
+            quantize_up(PARKED, lo)
+        for pair in pairs(OPEN):
+            for i in pair:
+                close(i, add_bias_scalar)
+            late_w4(PAIR)
+        for lo in (0, HALF):
+            cast_up(nc.scalar.copy, LATE, lo, lo + HALF)
+        for lo, pair in zip((0, HALF), pairs(PARKED)):
+            for i in pair:
+                close_parked(i)
+            quantize_up(LATE, lo)
+        late_w4(len(late_passes) - PAIR)
+        for first, second in pairs(LATE):
+            close(first, add_bias_scalar)
+            close(second, add_bias_vector)
+            late_w4(len(late_passes))

@@ -21,18 +21,22 @@ PACK = 4
 K_PASS = P * PACK
 PASSES = K // K_PASS
 N_TILES = N // P
-GROUP = 4
-GW = GROUP * P
-PARKED, OPEN, LATE = 0, 1, 2
-EARLY = 2 * GROUP
+BANKS = 8
 TQ = T // PACK
 
-HALF = GW // 2
-PAIR = 2
+OPEN = range(0, 4)
+PARKED = range(4, 9)
+LATE = range(9, 12)
+EARLY = LATE.start
+PART = 4
+PART_ORDER = (0, 2, 1)
 
 X_SPLIT = 352
 DOWN_SPLIT = 48
-LEAD = 5
+LAST_SPLITS = (88, 64)
+LAST_PART_SHARE = 96
+LEAD = 7
+FILL = 2
 
 
 def tile_mix_lowrank_fm_bias_kernel(tc, x, w4_words, w4_scales, down, up, b, out):
@@ -48,6 +52,7 @@ def tile_mix_lowrank_fm_bias_kernel(tc, x, w4_words, w4_scales, down, up, b, out
         def bank(number, name):
             return psum.tile([P, T], F32, name=name, tag=f"bank{number}")
 
+        parts = range(N_TILES // PART)
         x_raw = [sbuf(f"x_raw{g}", [P, PACK, T], F32) for g in range(PASSES)]
         x_bf = [sbuf(f"x_bf{g}", [P, T, PACK], BF16) for g in range(PASSES)]
         x_codes = [sbuf(f"x_codes{g}", [P, T], U32) for g in range(PASSES)]
@@ -56,14 +61,14 @@ def tile_mix_lowrank_fm_bias_kernel(tc, x, w4_words, w4_scales, down, up, b, out
         d_bf = [sbuf(f"d_bf{g}", [P, PACK, P, PACK], BF16) for g in range(PASSES)]
         d_codes = [sbuf(f"d_codes{g}", [P, R], U32) for g in range(PASSES)]
         d_scales = [sbuf(f"d_scales{g}", [P, R], U8) for g in range(PASSES)]
-        u_raw = [sbuf(f"u_raw{c}", [P, PACK, GW], F32) for c in (PARKED, OPEN, LATE)]
-        u_bf = [sbuf(f"u_bf{c}", [P, GW, PACK], BF16) for c in (PARKED, OPEN, LATE)]
-        u_codes = [sbuf(f"u_codes{c}", [P, GW], U32) for c in (PARKED, OPEN, LATE)]
-        u_scales = [sbuf(f"u_scales{c}", [P, GW], U8) for c in (PARKED, OPEN, LATE)]
+        u_raw = [sbuf(f"u_raw{c}", [P, PACK, PART * P], F32) for c in parts]
+        u_bf = [sbuf(f"u_bf{c}", [P, PART * P, PACK], BF16) for c in parts]
+        u_codes = [sbuf(f"u_codes{c}", [P, PART * P], U32) for c in parts]
+        u_scales = [sbuf(f"u_scales{c}", [P, PART * P], U8) for c in parts]
         w_early = sbuf("w_early", [P, PASSES, 2 * EARLY * P], U8)
-        w_late = sbuf("w_late", [P, PASSES, 2 * GW], U8)
+        w_late = sbuf("w_late", [P, PASSES, 2 * len(LATE) * P], U8)
         s_early = [sbuf(f"s_early{half}", [P, PASSES // 2, EARLY * P], U8) for half in range(2)]
-        s_late = sbuf("s_late", [P, PASSES, GW], U8)
+        s_late = sbuf("s_late", [P, PASSES, len(LATE) * P], U8)
         h_bf = sbuf("h_bf", [P, T, PACK], BF16)
         h_codes = sbuf("h_codes", [P, T], U32)
         h_scales = sbuf("h_scales", [P, T], U8)
@@ -101,10 +106,11 @@ def tile_mix_lowrank_fm_bias_kernel(tc, x, w4_words, w4_scales, down, up, b, out
             load_rows(x_raw[g], x[k_rows[g], :])
         for g in range(PASSES):
             load_rows(d_raw[g], down[k_rows[g], :])
-        for c in (OPEN, PARKED, LATE):
-            load_rows(u_raw[c], up[:, c * GW : (c + 1) * GW])
-            if c == OPEN:
-                load_w_words(w_late, EARLY * P, N)
+        load_w_words(w_late, EARLY * P, N)
+        for c in PART_ORDER:
+            load_rows(u_raw[c], up[:, c * PART * P : (c + 1) * PART * P])
+
+        on_vector, on_scalar = nc.vector.tensor_copy, nc.scalar.copy
 
         def interleave(copy, dst, src, lo, hi):
             copy(
@@ -124,6 +130,14 @@ def tile_mix_lowrank_fm_bias_kernel(tc, x, w4_words, w4_scales, down, up, b, out
         def quantize_cols(codes, scales, grouped, lo, hi):
             quantize(codes[:, lo:hi], scales[:, lo:hi], grouped[:, lo:hi, :].rearrange("p w j -> p (w j)"))
 
+        def cast_up(copy, first, count):
+            c, lo = first // PART, first % PART * P
+            interleave(copy, u_bf[c], u_raw[c], lo, lo + count * P)
+
+        def quantize_up(first, count):
+            c, lo = first // PART, first % PART * P
+            quantize_cols(u_codes[c], u_scales[c], u_bf[c], lo, lo + count * P)
+
         def w4_pass(i, g, stop):
             if i < EARLY:
                 words, scales, col = w_early, s_early[g // 2][:, g % 2, :], i * P
@@ -140,7 +154,7 @@ def tile_mix_lowrank_fm_bias_kernel(tc, x, w4_words, w4_scales, down, up, b, out
             )
 
         def up_pass(i, start):
-            c, col = i // GROUP, i % GROUP * P
+            c, col = i // PART, i % PART * P
             nc.tensor.matmul_mx(
                 out=acc[i][:],
                 lhsT=u_codes[c][:, col : col + P].bitcast(E4M3X4),
@@ -164,116 +178,116 @@ def tile_mix_lowrank_fm_bias_kernel(tc, x, w4_words, w4_scales, down, up, b, out
                 stop=(g == PASSES - 1 and a == PACK - 1),
             )
 
-        def add_bias_scalar(i):
-            nc.scalar.activation(out=y_sb[i][:], in_=acc[i][:], func=IDENTITY, bias=b_cols[:, i : i + 1])
+        def h_out(copy, q):
+            copy(out=h_bf[:, q * TQ : (q + 1) * TQ, :], in_=h_acc[q][:].rearrange("p (a n) -> p n a", a=PACK))
 
-        def add_bias_vector(i):
-            nc.vector.tensor_scalar_add(out=y_sb[i][:], in0=acc[i][:], scalar1=b_cols[:, i : i + 1])
+        def add_bias(i):
+            nc.scalar.activation(out=y_sb[i][:], in_=acc[i][:], func=IDENTITY, bias=b_cols[:, i : i + 1])
 
         def store(i):
             nc.sync.dma_start(out=out[i * P : (i + 1) * P, :], in_=y_sb[i][:])
 
-        def cast_up(copy, c, lo, hi):
-            interleave(copy, u_bf[c], u_raw[c], lo, hi)
-
-        def quantize_up(c, lo):
-            quantize_cols(u_codes[c], u_scales[c], u_bf[c], lo, lo + HALF)
-
-        def tiles(c):
-            return list(range(c * GROUP, (c + 1) * GROUP))
-
-        b_psum = bank(EARLY - 1, "b_psum")
-        nc.tensor.transpose(b_psum[:, 0:P], b_rows[:], ident[:])
-        nc.scalar.activation(out=b_cols[:], in_=b_psum[:, 0:N_TILES], func=IDENTITY)
-
-        acc = {i: bank(i, f"y{i}") for i in range(EARLY)}
-        for g in range(PASSES):
-            interleave(nc.vector.tensor_copy, x_bf[g], x_raw[g], 0, X_SPLIT)
-            interleave(nc.scalar.copy, x_bf[g], x_raw[g], X_SPLIT, T)
-            quantize_cols(x_codes[g], x_scales[g], x_bf[g], 0, T)
-            for i in tiles(PARKED):
-                w4_pass(i, g, stop=(g == PASSES - 1))
-            if g < PASSES // 2:
-                for i in tiles(OPEN):
-                    w4_pass(i, g, stop=False)
-        for g in range(PASSES // 2, PASSES):
-            for i in tiles(OPEN):
-                w4_pass(i, g, stop=False)
-        for i in tiles(PARKED):
-            add_bias_scalar(i)
-
-        h_acc = [bank(q, f"h{q}") for q in range(PACK)]
-        for g in range(PASSES):
-            permute(nc.vector.tensor_copy, g, 0, 0, P)
-            if g < PASSES // 2:
-                permute(nc.vector.tensor_copy, g, 2, 0, P)
-            elif g < PASSES - 1:
-                permute(nc.vector.tensor_copy, g, 2, 0, DOWN_SPLIT)
-                permute(nc.scalar.copy, g, 2, DOWN_SPLIT, P)
-            else:
-                permute(nc.scalar.copy, g, 2, 0, P)
-            if g < PASSES - 1:
-                quantize(d_codes[g][:], d_scales[g][:], d_bf[g][:].rearrange("p a m j -> p (a m j)"))
-            else:
-                for a in range(PACK):
-                    cols = slice(a * P, (a + 1) * P)
-                    quantize(d_codes[g][:, cols], d_scales[g][:, cols], d_bf[g][:, a, :, :].rearrange("p m j -> p (m j)"))
-            for parts in ((0,), (1,), (2, 3)):
-                for q in range(PACK):
-                    for a in parts:
-                        h_pass(g, a, q)
-
-        cast_up(nc.vector.tensor_copy, OPEN, 0, HALF)
-        for q in range(PACK):
-            copy = nc.vector.tensor_copy if q == PACK - 1 else nc.scalar.copy
-            copy(out=h_bf[:, q * TQ : (q + 1) * TQ, :], in_=h_acc[q][:].rearrange("p (a n) -> p n a", a=PACK))
-        quantize_up(OPEN, 0)
-        quantize_cols(h_codes, h_scales, h_bf, 0, T // 2)
-        quantize_cols(h_codes, h_scales, h_bf, T // 2, T)
-        cast_up(nc.scalar.copy, OPEN, HALF, HALF + P)
-        cast_up(nc.vector.tensor_copy, OPEN, HALF + P, GW)
-        quantize_up(OPEN, HALF)
-
-        late_passes = [(i, g) for i in tiles(LATE) for g in range(PASSES)]
-
-        def late_w4(count):
-            for i, g in late_passes[:count]:
-                if g == 0:
-                    acc[i] = bank(i - EARLY, f"y{i}")
-                w4_pass(i, g, stop=False)
-                late_passes.remove((i, g))
-
-        def close(i, add_bias):
+        def close(i):
             up_pass(i, start=False)
             add_bias(i)
             store(i)
 
-        def close_parked(i):
-            acc[i] = bank(GROUP + i, f"z{i}")
+        def close_parked(i, number):
+            acc[i] = bank(number, f"z{i}")
             up_pass(i, start=True)
             nc.vector.tensor_tensor(out=y_sb[i][:], in0=acc[i][:], in1=y_sb[i][:], op=ADD)
             store(i)
 
-        def pairs(c):
-            return [tiles(c)[first : first + PAIR] for first in range(0, GROUP, PAIR)]
+        b_psum = bank(BANKS - 1, "b_psum")
+        nc.tensor.transpose(b_psum[:, 0:P], b_rows[:], ident[:])
+        nc.scalar.activation(out=b_cols[:], in_=b_psum[:, 0:N_TILES], func=IDENTITY)
 
-        late_w4(LEAD)
-        for lo in (0, HALF):
-            cast_up(nc.vector.tensor_copy, PARKED, lo, lo + HALF)
-        for lo in (0, HALF):
-            quantize_up(PARKED, lo)
-        for pair in pairs(OPEN):
+        swept = list(PARKED) + list(OPEN[:-1])
+        home = {i: number for number, i in enumerate(swept)}
+        home[OPEN[-1]] = home[PARKED[-1]]
+        for i in LATE:
+            home[i] = i - EARLY
+        acc = {i: bank(home[i], f"y{i}") for i in swept}
+        for g in range(PASSES):
+            interleave(on_vector, x_bf[g], x_raw[g], 0, X_SPLIT)
+            interleave(on_scalar, x_bf[g], x_raw[g], X_SPLIT, T)
+            quantize_cols(x_codes[g], x_scales[g], x_bf[g], 0, T)
+            for i in swept:
+                w4_pass(i, g, stop=(i in PARKED and g == PASSES - 1))
+        for i in PARKED:
+            add_bias(i)
+
+        waiting = [(i, g) for i in [OPEN[-1], *LATE] for g in range(PASSES)]
+
+        def fill(count):
+            for i, g in waiting[:count]:
+                if g == 0:
+                    acc[i] = bank(home[i], f"y{i}")
+                w4_pass(i, g, stop=False)
+                waiting.remove((i, g))
+
+        h_acc = [bank(q, f"h{q}") for q in range(PACK)]
+        for g in range(PASSES - 1):
+            permute(on_vector, g, 0, 0, P)
+            if g < PASSES // 2:
+                permute(on_vector, g, 2, 0, P)
+            else:
+                permute(on_vector, g, 2, 0, DOWN_SPLIT)
+                permute(on_scalar, g, 2, DOWN_SPLIT, P)
+            quantize(d_codes[g][:], d_scales[g][:], d_bf[g][:].rearrange("p a m j -> p (a m j)"))
+            for a in range(PACK):
+                for q in range(PACK):
+                    h_pass(g, a, q)
+            if g < PASSES // 2:
+                fill(1)
+        g = PASSES - 1
+        for a, split in zip((0, 2), LAST_SPLITS):
+            permute(on_vector, g, a, 0, split)
+            permute(on_scalar, g, a, split, P)
+        for a in range(PACK):
+            cols = slice(a * P, (a + 1) * P)
+            quantize(d_codes[g][:, cols], d_scales[g][:, cols], d_bf[g][:, a, :, :].rearrange("p m j -> p (m j)"))
+        for h_parts in ((0,), (1,), (2, 3)):
+            for q in range(PACK):
+                for a in h_parts:
+                    h_pass(g, a, q)
+
+        for q in range(PACK):
+            h_out(on_scalar if q % 2 else on_vector, q)
+        cast_up(on_scalar, OPEN[1], 1)
+        cast_up(on_scalar, OPEN[2], 1)
+        quantize_cols(h_codes, h_scales, h_bf, 0, T // 2)
+        cast_up(on_vector, OPEN[0], 1)
+        quantize_cols(h_codes, h_scales, h_bf, T // 2, T)
+        quantize_up(OPEN[0], 1)
+        quantize_up(OPEN[1], 1)
+        cast_up(on_vector, OPEN[3], 1)
+        quantize_up(OPEN[2], 1)
+        quantize_up(OPEN[3], 1)
+        for count, pair in ((LEAD, OPEN[:2]), (FILL, OPEN[2:])):
+            fill(count)
             for i in pair:
-                close(i, add_bias_scalar)
-            late_w4(PAIR)
-        for lo in (0, HALF):
-            cast_up(nc.scalar.copy, LATE, lo, lo + HALF)
-        for lo, pair in zip((0, HALF), pairs(PARKED)):
-            for i in pair:
-                close_parked(i)
-            quantize_up(LATE, lo)
-        late_w4(len(late_passes) - PAIR)
-        for first, second in pairs(LATE):
-            close(first, add_bias_scalar)
-            close(second, add_bias_vector)
-            late_w4(len(late_passes))
+                close(i)
+
+        def make_part(c, end):
+            first = c * PART
+            cast_up(on_vector, first, 1)
+            cast_up(on_vector, first + 1, 1)
+            quantize_up(first, 1)
+            interleave(on_vector, u_bf[c], u_raw[c], 2 * P, end)
+            quantize_up(first + 1, 1)
+            quantize_up(first + 2, 2)
+
+        second, third = PART_ORDER[1:]
+        vector_end = PART * P - LAST_PART_SHARE
+        make_part(second, PART * P)
+        fill(FILL)
+        close_parked(PARKED[-1], len(LATE))
+        interleave(on_scalar, u_bf[third], u_raw[third], vector_end, PART * P)
+        for i in LATE:
+            fill(1 if i < LATE[-1] else len(waiting))
+            close(i)
+
+        make_part(third, vector_end)
+        for i in PARKED[:-1]:
+            close_parked(i, home[i - PART])

@@ -47,7 +47,7 @@ def tile_mix_lowrank_fm_bias_kernel(tc, x, w4_words, w4_scales, down, up, b, out
         ctx.enter_context(tc.manual_schedule())
 
         def sbuf(name, shape, dtype):
-            return keep.tile(shape, dtype, name=name, align_bytes=64)
+            return keep.tile(shape, dtype, name=name, align_bytes=256)
 
         def bank(number, name):
             return psum.tile([P, T], F32, name=name, tag=f"bank{number}")

@@ -22,20 +22,20 @@ K_PASS = P * PACK
 PASSES = K // K_PASS
 N_TILES = N // P
 BANKS = 8
+DMA_ALIGN = 256
 TQ = T // PACK
 
-OPEN = range(0, 4)
-PARKED = range(4, 9)
-LATE = range(9, 12)
+PARKED = range(0, 5)
+OPEN = range(5, 8)
+LATE = range(8, 12)
 EARLY = LATE.start
-PART = 4
-PART_ORDER = (0, 2, 1)
+PARTS = (range(5, 9), range(0, 1), range(9, 12), range(1, 5))
 
 X_SPLIT = 352
 DOWN_SPLIT = 48
-LAST_SPLITS = (88, 64)
+FIRST_HALF_SPLIT = 56
+SECOND_HALF_SPLITS = (88, 72)
 LAST_PART_SHARE = 96
-LEAD = 7
 FILL = 2
 
 
@@ -47,24 +47,25 @@ def tile_mix_lowrank_fm_bias_kernel(tc, x, w4_words, w4_scales, down, up, b, out
         ctx.enter_context(tc.manual_schedule())
 
         def sbuf(name, shape, dtype):
-            return keep.tile(shape, dtype, name=name, align_bytes=256)
+            return keep.tile(shape, dtype, name=name, align_bytes=DMA_ALIGN)
 
         def bank(number, name):
             return psum.tile([P, T], F32, name=name, tag=f"bank{number}")
 
-        parts = range(N_TILES // PART)
         x_raw = [sbuf(f"x_raw{g}", [P, PACK, T], F32) for g in range(PASSES)]
         x_bf = [sbuf(f"x_bf{g}", [P, T, PACK], BF16) for g in range(PASSES)]
         x_codes = [sbuf(f"x_codes{g}", [P, T], U32) for g in range(PASSES)]
         x_scales = [sbuf(f"x_scales{g}", [P, T], U8) for g in range(PASSES)]
-        d_raw = [sbuf(f"d_raw{g}", [P, PACK, R], F32) for g in range(PASSES)]
+        d_raw = [sbuf(f"d_raw{g}", [P, PACK, R], F32) for g in range(PASSES - 1)]
+        d_last = [sbuf(f"d_half{u}", [P, 2, R], F32) for u in range(2)]
         d_bf = [sbuf(f"d_bf{g}", [P, PACK, P, PACK], BF16) for g in range(PASSES)]
         d_codes = [sbuf(f"d_codes{g}", [P, R], U32) for g in range(PASSES)]
         d_scales = [sbuf(f"d_scales{g}", [P, R], U8) for g in range(PASSES)]
-        u_raw = [sbuf(f"u_raw{c}", [P, PACK, PART * P], F32) for c in parts]
-        u_bf = [sbuf(f"u_bf{c}", [P, PART * P, PACK], BF16) for c in parts]
-        u_codes = [sbuf(f"u_codes{c}", [P, PART * P], U32) for c in parts]
-        u_scales = [sbuf(f"u_scales{c}", [P, PART * P], U8) for c in parts]
+        u_raw = [sbuf(f"u_raw{c}", [P, PACK, len(part) * P], F32) for c, part in enumerate(PARTS)]
+        u_bf = [sbuf(f"u_bf{c}", [P, len(part) * P, PACK], BF16) for c, part in enumerate(PARTS)]
+        u_codes = [sbuf(f"u_codes{c}", [P, len(part) * P], U32) for c, part in enumerate(PARTS)]
+        u_scales = [sbuf(f"u_scales{c}", [P, len(part) * P], U8) for c, part in enumerate(PARTS)]
+        place = {i: (c, (i - part.start) * P) for c, part in enumerate(PARTS) for i in part}
         w_early = sbuf("w_early", [P, PASSES, 2 * EARLY * P], U8)
         w_late = sbuf("w_late", [P, PASSES, 2 * len(LATE) * P], U8)
         s_early = [sbuf(f"s_early{half}", [P, PASSES // 2, EARLY * P], U8) for half in range(2)]
@@ -104,11 +105,14 @@ def tile_mix_lowrank_fm_bias_kernel(tc, x, w4_words, w4_scales, down, up, b, out
         load_w_words(w_early, 0, EARLY * P)
         for g in range(1, PASSES):
             load_rows(x_raw[g], x[k_rows[g], :])
-        for g in range(PASSES):
+        for g in range(PASSES - 1):
             load_rows(d_raw[g], down[k_rows[g], :])
+        last_rows = down[k_rows[-1], :].rearrange("(p j) w -> p j w", j=PACK)
+        for u in range(2):
+            nc.sync.dma_start(out=d_last[u][:], in_=last_rows[:, 2 * u : 2 * u + 2, :])
         load_w_words(w_late, EARLY * P, N)
-        for c in PART_ORDER:
-            load_rows(u_raw[c], up[:, c * PART * P : (c + 1) * PART * P])
+        for c, part in enumerate(PARTS):
+            load_rows(u_raw[c], up[:, part.start * P : part.stop * P])
 
         on_vector, on_scalar = nc.vector.tensor_copy, nc.scalar.copy
 
@@ -124,6 +128,12 @@ def tile_mix_lowrank_fm_bias_kernel(tc, x, w4_words, w4_scales, down, up, b, out
                 in_=d_raw[g][:, :, 4 * lo : 4 * hi].rearrange("p j (m a) -> p m j a", a=4)[:, :, :, a : a + 2],
             )
 
+        def permute_half(copy, u, a, count, lo, hi):
+            copy(
+                out=d_bf[-1][:, a : a + count, lo:hi, 2 * u : 2 * u + 2].rearrange("p a m j -> p m j a"),
+                in_=d_last[u][:, :, 4 * lo : 4 * hi].rearrange("p j (m a) -> p m j a", a=4)[:, :, :, a : a + count],
+            )
+
         def quantize(codes, scales, grouped):
             nc.vector.quantize_mx(out=codes.bitcast(E4M3X4), scales=scales, in_=grouped)
 
@@ -131,11 +141,11 @@ def tile_mix_lowrank_fm_bias_kernel(tc, x, w4_words, w4_scales, down, up, b, out
             quantize(codes[:, lo:hi], scales[:, lo:hi], grouped[:, lo:hi, :].rearrange("p w j -> p (w j)"))
 
         def cast_up(copy, first, count):
-            c, lo = first // PART, first % PART * P
+            c, lo = place[first]
             interleave(copy, u_bf[c], u_raw[c], lo, lo + count * P)
 
         def quantize_up(first, count):
-            c, lo = first // PART, first % PART * P
+            c, lo = place[first]
             quantize_cols(u_codes[c], u_scales[c], u_bf[c], lo, lo + count * P)
 
         def w4_pass(i, g, stop):
@@ -154,7 +164,7 @@ def tile_mix_lowrank_fm_bias_kernel(tc, x, w4_words, w4_scales, down, up, b, out
             )
 
         def up_pass(i, start):
-            c, col = i // PART, i % PART * P
+            c, col = place[i]
             nc.tensor.matmul_mx(
                 out=acc[i][:],
                 lhsT=u_codes[c][:, col : col + P].bitcast(E4M3X4),
@@ -202,11 +212,11 @@ def tile_mix_lowrank_fm_bias_kernel(tc, x, w4_words, w4_scales, down, up, b, out
         nc.tensor.transpose(b_psum[:, 0:P], b_rows[:], ident[:])
         nc.scalar.activation(out=b_cols[:], in_=b_psum[:, 0:N_TILES], func=IDENTITY)
 
-        swept = list(PARKED) + list(OPEN[:-1])
-        home = {i: number for number, i in enumerate(swept)}
-        home[OPEN[-1]] = home[PARKED[-1]]
-        for i in LATE:
-            home[i] = i - EARLY
+        swept = list(PARKED) + list(OPEN)
+        home = {i: i for i in swept}
+        home[LATE[0]] = PARKED[-1]
+        for i in LATE[1:]:
+            home[i] = i - LATE[1]
         acc = {i: bank(home[i], f"y{i}") for i in swept}
         for g in range(PASSES):
             interleave(on_vector, x_bf[g], x_raw[g], 0, X_SPLIT)
@@ -217,7 +227,7 @@ def tile_mix_lowrank_fm_bias_kernel(tc, x, w4_words, w4_scales, down, up, b, out
         for i in PARKED:
             add_bias(i)
 
-        waiting = [(i, g) for i in [OPEN[-1], *LATE] for g in range(PASSES)]
+        waiting = [(i, g) for i in LATE for g in range(PASSES)]
 
         def fill(count):
             for i, g in waiting[:count]:
@@ -238,12 +248,12 @@ def tile_mix_lowrank_fm_bias_kernel(tc, x, w4_words, w4_scales, down, up, b, out
             for a in range(PACK):
                 for q in range(PACK):
                     h_pass(g, a, q)
-            if g < PASSES // 2:
-                fill(1)
         g = PASSES - 1
-        for a, split in zip((0, 2), LAST_SPLITS):
-            permute(on_vector, g, a, 0, split)
-            permute(on_scalar, g, a, split, P)
+        permute_half(on_vector, 0, 0, PACK, 0, FIRST_HALF_SPLIT)
+        permute_half(on_scalar, 0, 0, PACK, FIRST_HALF_SPLIT, P)
+        for a, split in zip((0, 2), SECOND_HALF_SPLITS):
+            permute_half(on_vector, 1, a, 2, 0, split)
+            permute_half(on_scalar, 1, a, 2, split, P)
         for a in range(PACK):
             cols = slice(a * P, (a + 1) * P)
             quantize(d_codes[g][:, cols], d_scales[g][:, cols], d_bf[g][:, a, :, :].rearrange("p m j -> p (m j)"))
@@ -252,42 +262,46 @@ def tile_mix_lowrank_fm_bias_kernel(tc, x, w4_words, w4_scales, down, up, b, out
                 for a in h_parts:
                     h_pass(g, a, q)
 
+        first, second, third, fourth = PARTS
         for q in range(PACK):
             h_out(on_scalar if q % 2 else on_vector, q)
-        cast_up(on_scalar, OPEN[1], 1)
-        cast_up(on_scalar, OPEN[2], 1)
+        cast_up(on_scalar, first[1], 1)
+        cast_up(on_scalar, first[2], 1)
         quantize_cols(h_codes, h_scales, h_bf, 0, T // 2)
-        cast_up(on_vector, OPEN[0], 1)
+        cast_up(on_vector, first[0], 1)
         quantize_cols(h_codes, h_scales, h_bf, T // 2, T)
-        quantize_up(OPEN[0], 1)
-        quantize_up(OPEN[1], 1)
-        cast_up(on_vector, OPEN[3], 1)
-        quantize_up(OPEN[2], 1)
-        quantize_up(OPEN[3], 1)
-        for count, pair in ((LEAD, OPEN[:2]), (FILL, OPEN[2:])):
+        quantize_up(first[0], 1)
+        quantize_up(first[1], 1)
+        cast_up(on_vector, first[3], 1)
+        quantize_up(first[2], 1)
+        quantize_up(first[3], 1)
+        for count, pair in ((2 * PASSES, first[:2]), (FILL, first[2:])):
             fill(count)
             for i in pair:
                 close(i)
 
-        def make_part(c, end):
-            first = c * PART
-            cast_up(on_vector, first, 1)
-            cast_up(on_vector, first + 1, 1)
-            quantize_up(first, 1)
-            interleave(on_vector, u_bf[c], u_raw[c], 2 * P, end)
-            quantize_up(first + 1, 1)
-            quantize_up(first + 2, 2)
-
-        second, third = PART_ORDER[1:]
-        vector_end = PART * P - LAST_PART_SHARE
-        make_part(second, PART * P)
+        tiles = [*second, *third]
+        cast_up(on_vector, tiles[0], 1)
+        for before, i in zip(tiles, tiles[1:]):
+            cast_up(on_vector, i, 1)
+            quantize_up(before, 1)
         fill(FILL)
-        close_parked(PARKED[-1], len(LATE))
-        interleave(on_scalar, u_bf[third], u_raw[third], vector_end, PART * P)
-        for i in LATE:
-            fill(1 if i < LATE[-1] else len(waiting))
-            close(i)
+        close_parked(second[0], PACK - 1)
+        quantize_up(tiles[-1], 1)
+        close(third[0])
+        last = len(PARTS) - 1
+        vector_end = len(fourth) * P - LAST_PART_SHARE
+        interleave(on_scalar, u_bf[last], u_raw[last], vector_end, len(fourth) * P)
+        fill(1)
+        close(third[1])
+        fill(len(waiting))
+        close(third[2])
 
-        make_part(third, vector_end)
-        for i in PARKED[:-1]:
-            close_parked(i, home[i - PART])
+        cast_up(on_vector, fourth[0], 1)
+        cast_up(on_vector, fourth[1], 1)
+        quantize_up(fourth[0], 1)
+        interleave(on_vector, u_bf[last], u_raw[last], 2 * P, vector_end)
+        quantize_up(fourth[1], 1)
+        quantize_up(fourth[2], 2)
+        for i, left in zip(fourth, first):
+            close_parked(i, home[left])

@@ -140,6 +140,11 @@ def tile_mix_lowrank_fm_bias_kernel(tc, x, w4_words, w4_scales, down, up, b, out
         def quantize_cols(codes, scales, grouped, lo, hi):
             quantize(codes[:, lo:hi], scales[:, lo:hi], grouped[:, lo:hi, :].rearrange("p w j -> p (w j)"))
 
+        def quantize_down(g, a, count):
+            cols = slice(a * P, (a + count) * P)
+            grouped = d_bf[g][:, a : a + count, :, :].rearrange("p a m j -> p (a m j)")
+            quantize(d_codes[g][:, cols], d_scales[g][:, cols], grouped)
+
         def cast_up(copy, first, count):
             c, lo = place[first]
             interleave(copy, u_bf[c], u_raw[c], lo, lo + count * P)
@@ -244,7 +249,9 @@ def tile_mix_lowrank_fm_bias_kernel(tc, x, w4_words, w4_scales, down, up, b, out
             else:
                 permute(on_vector, g, 2, 0, DOWN_SPLIT)
                 permute(on_scalar, g, 2, DOWN_SPLIT, P)
-            quantize(d_codes[g][:], d_scales[g][:], d_bf[g][:].rearrange("p a m j -> p (a m j)"))
+            step = PACK if g < PASSES // 2 else 2
+            for a in range(0, PACK, step):
+                quantize_down(g, a, step)
             for a in range(PACK):
                 for q in range(PACK):
                     h_pass(g, a, q)
@@ -255,12 +262,13 @@ def tile_mix_lowrank_fm_bias_kernel(tc, x, w4_words, w4_scales, down, up, b, out
             permute_half(on_vector, 1, a, 2, 0, split)
             permute_half(on_scalar, 1, a, 2, split, P)
         for a in range(PACK):
-            cols = slice(a * P, (a + 1) * P)
-            quantize(d_codes[g][:, cols], d_scales[g][:, cols], d_bf[g][:, a, :, :].rearrange("p m j -> p (m j)"))
-        for h_parts in ((0,), (1,), (2, 3)):
-            for q in range(PACK):
-                for a in h_parts:
-                    h_pass(g, a, q)
+            quantize_down(g, a, 1)
+        for a in range(PACK):
+            for q in (0, 1):
+                h_pass(g, a, q)
+        for q in (2, 3):
+            for a in range(PACK):
+                h_pass(g, a, q)
 
         first, second, third, fourth = PARTS
         for q in range(PACK):

@@ -1,7 +1,6 @@
 from contextlib import ExitStack
 
 import concourse.mybir as mybir
-from concourse.masks import make_identity
 
 K, R, N, T = 2048, 512, 1536, 512
 FLOPS = 2 * T * (K * R + K * N + R * N)
@@ -17,11 +16,11 @@ IDENTITY = mybir.ActivationFunctionType.Identity
 ADD = mybir.AluOpType.add
 
 P = 128
+QUAD = 32
 PACK = 4
 K_PASS = P * PACK
 PASSES = K // K_PASS
 N_TILES = N // P
-BANKS = 8
 DMA_ALIGN = 256
 TQ = T // PACK
 
@@ -29,14 +28,13 @@ PARKED = range(0, 5)
 OPEN = range(5, 8)
 LATE = range(8, 12)
 EARLY = LATE.start
-PARTS = (range(5, 9), range(0, 1), range(9, 12), range(1, 5))
+PARTS = (OPEN, LATE, PARKED[:2], PARKED[2:])
 
 X_SPLIT = 352
 DOWN_SPLIT = 48
 FIRST_HALF_SPLIT = 56
 SECOND_HALF_SPLITS = (88, 72)
-LAST_PART_SHARE = 96
-FILL = 2
+LEAD = 7
 
 
 def tile_mix_lowrank_fm_bias_kernel(tc, x, w4_words, w4_scales, down, up, b, out):
@@ -62,26 +60,25 @@ def tile_mix_lowrank_fm_bias_kernel(tc, x, w4_words, w4_scales, down, up, b, out
         d_codes = [sbuf(f"d_codes{g}", [P, R], U32) for g in range(PASSES)]
         d_scales = [sbuf(f"d_scales{g}", [P, R], U8) for g in range(PASSES)]
         u_raw = [sbuf(f"u_raw{c}", [P, PACK, len(part) * P], F32) for c, part in enumerate(PARTS)]
-        u_bf = [sbuf(f"u_bf{c}", [P, len(part) * P, PACK], BF16) for c, part in enumerate(PARTS)]
-        u_codes = [sbuf(f"u_codes{c}", [P, len(part) * P], U32) for c, part in enumerate(PARTS)]
-        u_scales = [sbuf(f"u_scales{c}", [P, len(part) * P], U8) for c, part in enumerate(PARTS)]
+        u_bf = sbuf("u_bf", [P, N, PACK], BF16)
+        u_codes = sbuf("u_codes", [P, N], U32)
+        u_scales = sbuf("u_scales", [P, N], U8)
         place = {i: (c, (i - part.start) * P) for c, part in enumerate(PARTS) for i in part}
         w_early = sbuf("w_early", [P, PASSES, 2 * EARLY * P], U8)
         w_late = sbuf("w_late", [P, PASSES, 2 * len(LATE) * P], U8)
-        s_early = [sbuf(f"s_early{half}", [P, PASSES // 2, EARLY * P], U8) for half in range(2)]
+        s_first = sbuf("s_first", [P, 1, EARLY * P], U8)
+        s_next = sbuf("s_next", [P, PASSES - 1, EARLY * P], U8)
         s_late = sbuf("s_late", [P, PASSES, len(LATE) * P], U8)
         h_bf = sbuf("h_bf", [P, T, PACK], BF16)
         h_codes = sbuf("h_codes", [P, T], U32)
         h_scales = sbuf("h_scales", [P, T], U8)
-        ident = sbuf("ident", [P, P], F32)
         b_rows = sbuf("b_rows", [P, P], F32)
-        b_cols = sbuf("b_cols", [P, N_TILES], F32)
+        b_cols = sbuf("b_cols", [P, P], F32)
         y_sb = [sbuf(f"y_sb{i}", [P, T], F32) for i in range(N_TILES)]
 
         nc.vector.memset(b_rows[:], 0.0)
-        for tile in (s_early[1], s_early[0], s_late):
+        for tile in (s_next, s_first, s_late):
             nc.vector.memset(tile[:].rearrange("p g n -> p (g n)").bitcast(I32), 0)
-        make_identity(nc, ident[:])
 
         def load_rows(tile, rows):
             nc.sync.dma_start(out=tile[:], in_=rows.rearrange("(p j) w -> p j w", j=PACK))
@@ -92,15 +89,15 @@ def tile_mix_lowrank_fm_bias_kernel(tc, x, w4_words, w4_scales, down, up, b, out
         def load_w_scales(queue, tile, passes, lo, hi):
             for s in range(4):
                 queue.dma_start(
-                    out=tile[s:P:32, :, :].bitcast(I32),
+                    out=tile[s:P:QUAD, :, :].bitcast(I32),
                     in_=w4_scales[passes, s:16:4, lo:hi].rearrange("g q n -> q g n").bitcast(I32),
                 )
 
         k_rows = [slice(g * K_PASS, (g + 1) * K_PASS) for g in range(PASSES)]
         load_rows(x_raw[0], x[k_rows[0], :])
         nc.scalar.dma_start(out=b_rows[0:N_TILES, :], in_=b.rearrange("(c p) -> c p", p=P))
-        load_w_scales(nc.sync, s_early[0], slice(0, PASSES // 2), 0, EARLY * P)
-        load_w_scales(nc.gpsimd, s_early[1], slice(PASSES // 2, PASSES), 0, EARLY * P)
+        load_w_scales(nc.sync, s_first, slice(0, 1), 0, EARLY * P)
+        load_w_scales(nc.gpsimd, s_next, slice(1, PASSES), 0, EARLY * P)
         load_w_scales(nc.gpsimd, s_late, slice(0, PASSES), EARLY * P, N)
         load_w_words(w_early, 0, EARLY * P)
         for g in range(1, PASSES):
@@ -116,10 +113,13 @@ def tile_mix_lowrank_fm_bias_kernel(tc, x, w4_words, w4_scales, down, up, b, out
 
         on_vector, on_scalar = nc.vector.tensor_copy, nc.scalar.copy
 
-        def interleave(copy, dst, src, lo, hi):
+        def by_activation(out, in_):
+            nc.scalar.activation(out=out, in_=in_, func=IDENTITY)
+
+        def interleave(copy, dst, src):
             copy(
-                out=dst[:, lo:hi, :].rearrange("p (c i) j -> p c j i", i=4),
-                in_=src[:, :, lo:hi].rearrange("p j (c i) -> p c j i", i=4),
+                out=dst.rearrange("p (c i) j -> p c j i", i=4),
+                in_=src.rearrange("p j (c i) -> p c j i", i=4),
             )
 
         def permute(copy, g, a, lo, hi):
@@ -145,22 +145,21 @@ def tile_mix_lowrank_fm_bias_kernel(tc, x, w4_words, w4_scales, down, up, b, out
             grouped = d_bf[g][:, a : a + count, :, :].rearrange("p a m j -> p (a m j)")
             quantize(d_codes[g][:, cols], d_scales[g][:, cols], grouped)
 
-        def cast_up(copy, first, count):
-            c, lo = place[first]
-            interleave(copy, u_bf[c], u_raw[c], lo, lo + count * P)
+        def cast_up(copy, i):
+            c, lo = place[i]
+            interleave(copy, u_bf[:, i * P : (i + 1) * P, :], u_raw[c][:, :, lo : lo + P])
 
-        def quantize_up(first, count):
-            c, lo = place[first]
-            quantize_cols(u_codes[c], u_scales[c], u_bf[c], lo, lo + count * P)
+        def quantize_up(i):
+            quantize_cols(u_codes, u_scales, u_bf, i * P, (i + 1) * P)
 
         def w4_pass(i, g, stop):
             if i < EARLY:
-                words, scales, col = w_early, s_early[g // 2][:, g % 2, :], i * P
+                words, scales, col = w_early[:, g, :], (s_next[:, g - 1, :] if g else s_first[:, 0, :]), i * P
             else:
-                words, scales, col = w_late, s_late[:, g, :], (i - EARLY) * P
+                words, scales, col = w_late[:, g, :], s_late[:, g, :], (i - EARLY) * P
             nc.tensor.matmul_mx(
                 out=acc[i][:],
-                lhsT=words[:, g, 2 * col : 2 * (col + P)].bitcast(E2M1X4),
+                lhsT=words[:, 2 * col : 2 * (col + P)].bitcast(E2M1X4),
                 lhsT_scale=scales[:, col : col + P],
                 rhs=x_codes[g][:].bitcast(E4M3X4),
                 rhs_scale=x_scales[g][:],
@@ -169,11 +168,11 @@ def tile_mix_lowrank_fm_bias_kernel(tc, x, w4_words, w4_scales, down, up, b, out
             )
 
         def up_pass(i, start):
-            c, col = place[i]
+            cols = slice(i * P, (i + 1) * P)
             nc.tensor.matmul_mx(
                 out=acc[i][:],
-                lhsT=u_codes[c][:, col : col + P].bitcast(E4M3X4),
-                lhsT_scale=u_scales[c][:, col : col + P],
+                lhsT=u_codes[:, cols].bitcast(E4M3X4),
+                lhsT_scale=u_scales[:, cols],
                 rhs=h_codes[:].bitcast(E4M3X4),
                 rhs_scale=h_scales[:],
                 start=start,
@@ -213,25 +212,34 @@ def tile_mix_lowrank_fm_bias_kernel(tc, x, w4_words, w4_scales, down, up, b, out
             nc.vector.tensor_tensor(out=y_sb[i][:], in0=acc[i][:], in1=y_sb[i][:], op=ADD)
             store(i)
 
-        b_psum = bank(BANKS - 1, "b_psum")
-        nc.tensor.transpose(b_psum[:, 0:P], b_rows[:], ident[:])
-        nc.scalar.activation(out=b_cols[:], in_=b_psum[:, 0:N_TILES], func=IDENTITY)
+        def bias_to_partitions():
+            nc.vector.transpose(out=b_cols[:], in_=b_rows[:])
+            for quad in range(QUAD, P, QUAD):
+                nc.vector.tensor_copy(
+                    out=b_cols[quad : quad + QUAD, 0:N_TILES].bitcast(I32),
+                    in_=b_cols[0:QUAD, quad : quad + N_TILES].bitcast(I32),
+                )
 
-        swept = list(PARKED) + list(OPEN)
-        home = {i: i for i in swept}
-        home[LATE[0]] = PARKED[-1]
-        for i in LATE[1:]:
-            home[i] = i - LATE[1]
-        acc = {i: bank(home[i], f"y{i}") for i in swept}
+        acc = {i: bank(i, f"y{i}") for i in range(EARLY)}
         for g in range(PASSES):
-            interleave(on_vector, x_bf[g], x_raw[g], 0, X_SPLIT)
-            interleave(on_scalar, x_bf[g], x_raw[g], X_SPLIT, T)
+            interleave(on_vector, x_bf[g][:, 0:X_SPLIT, :], x_raw[g][:, :, 0:X_SPLIT])
+            interleave(by_activation if g == 0 else on_scalar, x_bf[g][:, X_SPLIT:T, :], x_raw[g][:, :, X_SPLIT:T])
             quantize_cols(x_codes[g], x_scales[g], x_bf[g], 0, T)
-            for i in swept:
+            if g == 0:
+                bias_to_partitions()
+
+        def sweep(tiles, g):
+            for i in tiles:
                 w4_pass(i, g, stop=(i in PARKED and g == PASSES - 1))
+
+        for tiles, passes in ((range(EARLY), (0, 1)), (PARKED, (2, 3)), (OPEN, (2, 3))):
+            for g in passes:
+                sweep(tiles, g)
         for i in PARKED:
             add_bias(i)
 
+        home = {i: i - LATE[1] for i in LATE[1:]}
+        home[LATE[0]] = PARKED[-1]
         waiting = [(i, g) for i in LATE for g in range(PASSES)]
 
         def fill(count):
@@ -270,46 +278,41 @@ def tile_mix_lowrank_fm_bias_kernel(tc, x, w4_words, w4_scales, down, up, b, out
             for a in range(PACK):
                 h_pass(g, a, q)
 
-        first, second, third, fourth = PARTS
         for q in range(PACK):
             h_out(on_scalar if q % 2 else on_vector, q)
-        cast_up(on_scalar, first[1], 1)
-        cast_up(on_scalar, first[2], 1)
+        for i in OPEN[1:]:
+            cast_up(on_scalar, i)
+        cast_up(on_vector, OPEN[0])
         quantize_cols(h_codes, h_scales, h_bf, 0, T // 2)
-        cast_up(on_vector, first[0], 1)
         quantize_cols(h_codes, h_scales, h_bf, T // 2, T)
-        quantize_up(first[0], 1)
-        quantize_up(first[1], 1)
-        cast_up(on_vector, first[3], 1)
-        quantize_up(first[2], 1)
-        quantize_up(first[3], 1)
-        for count, pair in ((2 * PASSES, first[:2]), (FILL, first[2:])):
-            fill(count)
-            for i in pair:
-                close(i)
+        for i in OPEN:
+            quantize_up(i)
+        fill(LEAD)
+        close(OPEN[0])
+        close(OPEN[1])
+        fill(2 * PASSES - LEAD)
+        close(OPEN[2])
 
-        tiles = [*second, *third]
-        cast_up(on_vector, tiles[0], 1)
+        tiles = [*LATE[:-1], *PARTS[2], LATE[-1]]
+        cast_up(on_vector, tiles[0])
         for before, i in zip(tiles, tiles[1:]):
-            cast_up(on_vector, i, 1)
-            quantize_up(before, 1)
-        fill(FILL)
-        close_parked(second[0], PACK - 1)
-        quantize_up(tiles[-1], 1)
-        close(third[0])
-        last = len(PARTS) - 1
-        vector_end = len(fourth) * P - LAST_PART_SHARE
-        interleave(on_scalar, u_bf[last], u_raw[last], vector_end, len(fourth) * P)
-        fill(1)
-        close(third[1])
-        fill(len(waiting))
-        close(third[2])
-
-        cast_up(on_vector, fourth[0], 1)
-        cast_up(on_vector, fourth[1], 1)
-        quantize_up(fourth[0], 1)
-        interleave(on_vector, u_bf[last], u_raw[last], 2 * P, vector_end)
-        quantize_up(fourth[1], 1)
-        quantize_up(fourth[2], 2)
-        for i, left in zip(fourth, first):
-            close_parked(i, home[left])
+            cast_up(on_vector, i)
+            quantize_up(before)
+        quantize_up(tiles[-1])
+        for count, i in zip((2, 1, 1), LATE[:-1]):
+            fill(count)
+            close(i)
+        last = PARTS[-1]
+        for i in last[1:]:
+            cast_up(on_scalar, i)
+        cast_up(on_vector, last[0])
+        close_parked(PARKED[0], PACK - 1)
+        quantize_up(last[0])
+        fill(PASSES // 2)
+        close_parked(PARKED[1], OPEN[0])
+        for i in last[1:]:
+            quantize_up(i)
+        fill(PASSES // 2)
+        close(LATE[-1])
+        for i, number in zip(last, (OPEN[1], OPEN[2], home[LATE[0]])):
+            close_parked(i, number)

@@ -145,9 +145,9 @@ def tile_mix_lowrank_fm_bias_kernel(tc, x, w4_words, w4_scales, down, up, b, out
             grouped = d_bf[g][:, a : a + count, :, :].rearrange("p a m j -> p (a m j)")
             quantize(d_codes[g][:, cols], d_scales[g][:, cols], grouped)
 
-        def cast_up(copy, i):
-            c, lo = place[i]
-            interleave(copy, u_bf[:, i * P : (i + 1) * P, :], u_raw[c][:, :, lo : lo + P])
+        def cast_up(copy, i, lo=0, hi=P):
+            c, col = place[i]
+            interleave(copy, u_bf[:, i * P + lo : i * P + hi, :], u_raw[c][:, :, col + lo : col + hi])
 
         def quantize_up(i):
             quantize_cols(u_codes, u_scales, u_bf, i * P, (i + 1) * P)
@@ -280,17 +280,19 @@ def tile_mix_lowrank_fm_bias_kernel(tc, x, w4_words, w4_scales, down, up, b, out
 
         for q in range(PACK):
             h_out(on_scalar if q % 2 else on_vector, q)
-        for i in OPEN[1:]:
-            cast_up(on_scalar, i)
-        cast_up(on_vector, OPEN[0])
+        cast_up(on_scalar, OPEN[0], P // 2, P)
+        cast_up(on_scalar, OPEN[1])
         quantize_cols(h_codes, h_scales, h_bf, 0, T // 2)
+        cast_up(on_vector, OPEN[0], 0, P // 2)
         quantize_cols(h_codes, h_scales, h_bf, T // 2, T)
-        for i in OPEN:
+        quantize_up(OPEN[0])
+        cast_up(on_vector, OPEN[2])
+        for i in OPEN[1:]:
             quantize_up(i)
         fill(LEAD)
         close(OPEN[0])
-        close(OPEN[1])
         fill(2 * PASSES - LEAD)
+        close(OPEN[1])
         close(OPEN[2])
 
         tiles = [*LATE[:-1], *PARTS[2], LATE[-1]]

from contextlib import ExitStack

import concourse.mybir as mybir

K, R, N, T = 2048, 512, 1536, 512
FLOPS = 2 * T * (K * R + K * N + R * N)

F32 = mybir.dt.float32
BF16 = mybir.dt.bfloat16
I32 = mybir.dt.int32
U32 = mybir.dt.uint32
U8 = mybir.dt.uint8
E4M3X4 = mybir.dt.float8_e4m3fn_x4
E2M1X4 = mybir.dt.float4_e2m1fn_x4
IDENTITY = mybir.ActivationFunctionType.Identity
ADD = mybir.AluOpType.add

P = 128
QUAD = 32
PACK = 4
K_PASS = P * PACK
PASSES = K // K_PASS
N_TILES = N // P
DMA_ALIGN = 256
TQ = T // PACK

PARKED = range(0, 5)
OPEN = range(5, 8)
LATE = range(8, 12)
EARLY = LATE.start
PARTS = (OPEN, LATE, PARKED[:2], PARKED[2:])

X_SPLIT = 352
DOWN_SPLIT = 48
FIRST_HALF_SPLIT = 56
SECOND_HALF_SPLITS = (88, 72)
LEAD = 7


def tile_mix_lowrank_fm_bias_kernel(tc, x, w4_words, w4_scales, down, up, b, out):
    nc = tc.nc
    with ExitStack() as ctx:
        keep = ctx.enter_context(tc.tile_pool(name="keep", bufs=1))
        psum = ctx.enter_context(tc.psum_pool(name="psum", bufs=1))
        ctx.enter_context(tc.manual_schedule())

        def sbuf(name, shape, dtype):
            return keep.tile(shape, dtype, name=name, align_bytes=DMA_ALIGN)

        def bank(number, name):
            return psum.tile([P, T], F32, name=name, tag=f"bank{number}")

        x_raw = [sbuf(f"x_raw{g}", [P, PACK, T], F32) for g in range(PASSES)]
        x_bf = [sbuf(f"x_bf{g}", [P, T, PACK], BF16) for g in range(PASSES)]
        x_codes = [sbuf(f"x_codes{g}", [P, T], U32) for g in range(PASSES)]
        x_scales = [sbuf(f"x_scales{g}", [P, T], U8) for g in range(PASSES)]
        d_raw = [sbuf(f"d_raw{g}", [P, PACK, R], F32) for g in range(PASSES - 1)]
        d_last = [sbuf(f"d_half{u}", [P, 2, R], F32) for u in range(2)]
        d_bf = [sbuf(f"d_bf{g}", [P, PACK, P, PACK], BF16) for g in range(PASSES)]
        d_codes = [sbuf(f"d_codes{g}", [P, R], U32) for g in range(PASSES)]
        d_scales = [sbuf(f"d_scales{g}", [P, R], U8) for g in range(PASSES)]
        u_raw = [sbuf(f"u_raw{c}", [P, PACK, len(part) * P], F32) for c, part in enumerate(PARTS)]
        u_bf = sbuf("u_bf", [P, N, PACK], BF16)
        u_codes = sbuf("u_codes", [P, N], U32)
        u_scales = sbuf("u_scales", [P, N], U8)
        place = {i: (c, (i - part.start) * P) for c, part in enumerate(PARTS) for i in part}
        w_early = sbuf("w_early", [P, PASSES, 2 * EARLY * P], U8)
        w_late = sbuf("w_late", [P, PASSES, 2 * len(LATE) * P], U8)
        s_first = sbuf("s_first", [P, 1, EARLY * P], U8)
        s_next = sbuf("s_next", [P, PASSES - 1, EARLY * P], U8)
        s_late = sbuf("s_late", [P, PASSES, len(LATE) * P], U8)
        h_bf = sbuf("h_bf", [P, T, PACK], BF16)
        h_codes = sbuf("h_codes", [P, T], U32)
        h_scales = sbuf("h_scales", [P, T], U8)
        b_rows = sbuf("b_rows", [P, P], F32)
        b_cols = sbuf("b_cols", [P, P], F32)
        y_sb = [sbuf(f"y_sb{i}", [P, T], F32) for i in range(N_TILES)]

        nc.vector.memset(b_rows[:], 0.0)
        for tile in (s_next, s_first, s_late):
            nc.vector.memset(tile[:].rearrange("p g n -> p (g n)").bitcast(I32), 0)

        def load_rows(tile, rows):
            nc.sync.dma_start(out=tile[:], in_=rows.rearrange("(p j) w -> p j w", j=PACK))

        def load_w_words(tile, lo, hi):
            nc.sync.dma_start(out=tile[:], in_=w4_words[:, :, 2 * lo : 2 * hi].rearrange("g p n -> p g n"))

        def load_w_scales(queue, tile, passes, lo, hi):
            for s in range(4):
                queue.dma_start(
                    out=tile[s:P:QUAD, :, :].bitcast(I32),
                    in_=w4_scales[passes, s:16:4, lo:hi].rearrange("g q n -> q g n").bitcast(I32),
                )

        k_rows = [slice(g * K_PASS, (g + 1) * K_PASS) for g in range(PASSES)]
        load_rows(x_raw[0], x[k_rows[0], :])
        nc.scalar.dma_start(out=b_rows[0:N_TILES, :], in_=b.rearrange("(c p) -> c p", p=P))
        load_w_scales(nc.sync, s_first, slice(0, 1), 0, EARLY * P)
        load_w_scales(nc.gpsimd, s_next, slice(1, PASSES), 0, EARLY * P)
        load_w_scales(nc.gpsimd, s_late, slice(0, PASSES), EARLY * P, N)
        load_w_words(w_early, 0, EARLY * P)
        for g in range(1, PASSES):
            load_rows(x_raw[g], x[k_rows[g], :])
        for g in range(PASSES - 1):
            load_rows(d_raw[g], down[k_rows[g], :])
        last_rows = down[k_rows[-1], :].rearrange("(p j) w -> p j w", j=PACK)
        for u in range(2):
            nc.sync.dma_start(out=d_last[u][:], in_=last_rows[:, 2 * u : 2 * u + 2, :])
        load_w_words(w_late, EARLY * P, N)
        for c, part in enumerate(PARTS):
            load_rows(u_raw[c], up[:, part.start * P : part.stop * P])

        on_vector, on_scalar = nc.vector.tensor_copy, nc.scalar.copy

        def by_activation(out, in_):
            nc.scalar.activation(out=out, in_=in_, func=IDENTITY)

        def interleave(copy, dst, src):
            copy(
                out=dst.rearrange("p (c i) j -> p c j i", i=4),
                in_=src.rearrange("p j (c i) -> p c j i", i=4),
            )

        def permute(copy, g, a, lo, hi):
            copy(
                out=d_bf[g][:, a : a + 2, lo:hi, :].rearrange("p a m j -> p m j a"),
                in_=d_raw[g][:, :, 4 * lo : 4 * hi].rearrange("p j (m a) -> p m j a", a=4)[:, :, :, a : a + 2],
            )

        def permute_half(copy, u, a, count, lo, hi):
            copy(
                out=d_bf[-1][:, a : a + count, lo:hi, 2 * u : 2 * u + 2].rearrange("p a m j -> p m j a"),
                in_=d_last[u][:, :, 4 * lo : 4 * hi].rearrange("p j (m a) -> p m j a", a=4)[:, :, :, a : a + count],
            )

        def quantize(codes, scales, grouped):
            nc.vector.quantize_mx(out=codes.bitcast(E4M3X4), scales=scales, in_=grouped)

        def quantize_cols(codes, scales, grouped, lo, hi):
            quantize(codes[:, lo:hi], scales[:, lo:hi], grouped[:, lo:hi, :].rearrange("p w j -> p (w j)"))

        def quantize_down(g, a, count):
            cols = slice(a * P, (a + count) * P)
            grouped = d_bf[g][:, a : a + count, :, :].rearrange("p a m j -> p (a m j)")
            quantize(d_codes[g][:, cols], d_scales[g][:, cols], grouped)

        def cast_up(copy, i, lo=0, hi=P):
            c, col = place[i]
            interleave(copy, u_bf[:, i * P + lo : i * P + hi, :], u_raw[c][:, :, col + lo : col + hi])

        def quantize_up(i):
            quantize_cols(u_codes, u_scales, u_bf, i * P, (i + 1) * P)

        def w4_pass(i, g, stop):
            if i < EARLY:
                words, scales, col = w_early[:, g, :], (s_next[:, g - 1, :] if g else s_first[:, 0, :]), i * P
            else:
                words, scales, col = w_late[:, g, :], s_late[:, g, :], (i - EARLY) * P
            nc.tensor.matmul_mx(
                out=acc[i][:],
                lhsT=words[:, 2 * col : 2 * (col + P)].bitcast(E2M1X4),
                lhsT_scale=scales[:, col : col + P],
                rhs=x_codes[g][:].bitcast(E4M3X4),
                rhs_scale=x_scales[g][:],
                start=(g == 0),
                stop=stop,
            )

        def up_pass(i, start):
            cols = slice(i * P, (i + 1) * P)
            nc.tensor.matmul_mx(
                out=acc[i][:],
                lhsT=u_codes[:, cols].bitcast(E4M3X4),
                lhsT_scale=u_scales[:, cols],
                rhs=h_codes[:].bitcast(E4M3X4),
                rhs_scale=h_scales[:],
                start=start,
                stop=True,
            )

        def h_pass(g, a, q):
            cols = slice(a * P, (a + 1) * P)
            ts = slice(q * TQ, (q + 1) * TQ)
            nc.tensor.matmul_mx(
                out=h_acc[q][:, a * TQ : (a + 1) * TQ],
                lhsT=d_codes[g][:, cols].bitcast(E4M3X4),
                lhsT_scale=d_scales[g][:, cols],
                rhs=x_codes[g][:, ts].bitcast(E4M3X4),
                rhs_scale=x_scales[g][:, ts],
                start=(g == 0 and a == 0),
                stop=(g == PASSES - 1 and a == PACK - 1),
            )

        def h_out(copy, q):
            copy(out=h_bf[:, q * TQ : (q + 1) * TQ, :], in_=h_acc[q][:].rearrange("p (a n) -> p n a", a=PACK))

        def add_bias(i):
            nc.scalar.activation(out=y_sb[i][:], in_=acc[i][:], func=IDENTITY, bias=b_cols[:, i : i + 1])

        def store(i):
            nc.sync.dma_start(out=out[i * P : (i + 1) * P, :], in_=y_sb[i][:])

        def close(i):
            up_pass(i, start=False)
            add_bias(i)
            store(i)

        def close_parked(i, number):
            acc[i] = bank(number, f"z{i}")
            up_pass(i, start=True)
            nc.vector.tensor_tensor(out=y_sb[i][:], in0=acc[i][:], in1=y_sb[i][:], op=ADD)
            store(i)

        def bias_to_partitions():
            nc.vector.transpose(out=b_cols[:], in_=b_rows[:])
            for quad in range(QUAD, P, QUAD):
                nc.vector.tensor_copy(
                    out=b_cols[quad : quad + QUAD, 0:N_TILES].bitcast(I32),
                    in_=b_cols[0:QUAD, quad : quad + N_TILES].bitcast(I32),
                )

        acc = {i: bank(i, f"y{i}") for i in range(EARLY)}
        for g in range(PASSES):
            interleave(on_vector, x_bf[g][:, 0:X_SPLIT, :], x_raw[g][:, :, 0:X_SPLIT])
            interleave(by_activation if g == 0 else on_scalar, x_bf[g][:, X_SPLIT:T, :], x_raw[g][:, :, X_SPLIT:T])
            quantize_cols(x_codes[g], x_scales[g], x_bf[g], 0, T)
            if g == 0:
                bias_to_partitions()

        def sweep(tiles, g):
            for i in tiles:
                w4_pass(i, g, stop=(i in PARKED and g == PASSES - 1))

        for tiles, passes in ((range(EARLY), (0, 1)), (PARKED, (2, 3)), (OPEN, (2, 3))):
            for g in passes:
                sweep(tiles, g)
        for i in PARKED:
            add_bias(i)

        home = {i: i - LATE[1] for i in LATE[1:]}
        home[LATE[0]] = PARKED[-1]
        waiting = [(i, g) for i in LATE for g in range(PASSES)]

        def fill(count):
            for i, g in waiting[:count]:
                if g == 0:
                    acc[i] = bank(home[i], f"y{i}")
                w4_pass(i, g, stop=False)
                waiting.remove((i, g))

        h_acc = [bank(q, f"h{q}") for q in range(PACK)]
        for g in range(PASSES - 1):
            permute(on_vector, g, 0, 0, P)
            if g < PASSES // 2:
                permute(on_vector, g, 2, 0, P)
            else:
                permute(on_vector, g, 2, 0, DOWN_SPLIT)
                permute(on_scalar, g, 2, DOWN_SPLIT, P)
            step = PACK if g < PASSES // 2 else 2
            for a in range(0, PACK, step):
                quantize_down(g, a, step)
            for a in range(PACK):
                for q in range(PACK):
                    h_pass(g, a, q)
        g = PASSES - 1
        permute_half(on_vector, 0, 0, PACK, 0, FIRST_HALF_SPLIT)
        permute_half(on_scalar, 0, 0, PACK, FIRST_HALF_SPLIT, P)
        for a, split in zip((0, 2), SECOND_HALF_SPLITS):
            permute_half(on_vector, 1, a, 2, 0, split)
            permute_half(on_scalar, 1, a, 2, split, P)
        for a in range(PACK):
            quantize_down(g, a, 1)
        for a in range(PACK):
            for q in (0, 1):
                h_pass(g, a, q)
        for q in (2, 3):
            for a in range(PACK):
                h_pass(g, a, q)

        for q in range(PACK):
            h_out(on_scalar if q % 2 else on_vector, q)
        cast_up(on_scalar, OPEN[0], P // 2, P)
        cast_up(on_scalar, OPEN[1])
        quantize_cols(h_codes, h_scales, h_bf, 0, T // 2)
        cast_up(on_vector, OPEN[0], 0, P // 2)
        quantize_cols(h_codes, h_scales, h_bf, T // 2, T)
        quantize_up(OPEN[0])
        cast_up(on_vector, OPEN[2])
        for i in OPEN[1:]:
            quantize_up(i)
        fill(LEAD)
        close(OPEN[0])
        fill(2 * PASSES - LEAD)
        close(OPEN[1])
        close(OPEN[2])

        tiles = [*LATE[:-1], *PARTS[2], LATE[-1]]
        cast_up(on_vector, tiles[0])
        for before, i in zip(tiles, tiles[1:]):
            cast_up(on_vector, i)
            quantize_up(before)
        quantize_up(tiles[-1])
        for count, i in zip((2, 1, 1), LATE[:-1]):
            fill(count)
            close(i)
        last = PARTS[-1]
        for i in last[1:]:
            cast_up(on_scalar, i)
        cast_up(on_vector, last[0])
        close_parked(PARKED[0], PACK - 1)
        quantize_up(last[0])
        fill(PASSES // 2)
        close_parked(PARKED[1], OPEN[0])
        for i in last[1:]:
            quantize_up(i)
        fill(PASSES // 2)
        close(LATE[-1])
        for i, number in zip(last, (OPEN[1], OPEN[2], home[LATE[0]])):
            close_parked(i, number)
